import numpy as np
import ml_dtypes


def mxq(x, axis, fmt="e4m3"):
    dtype, down = {"e4m3": (ml_dtypes.float8_e4m3fn, 7), "e5m2": (ml_dtypes.float8_e5m2, 14)}[fmt]
    v = np.moveaxis(np.asarray(x, np.float32).astype(ml_dtypes.bfloat16).astype(np.float64), axis, -1)
    blocks = v.reshape(v.shape[:-1] + (-1, 32))
    amax = np.abs(blocks).max(-1, keepdims=True)
    byte = np.maximum(np.where(amax > 0, np.frexp(amax)[1] - 1 + 127, 0) - down, 1)
    scale = np.exp2(byte - 127.0)
    codes = (blocks / scale).astype(np.float32).astype(dtype).astype(np.float64)
    return np.moveaxis((codes * scale).reshape(v.shape), -1, axis)


WIDE = False


def mx_kscale(k):
    if not WIDE:
        return np.ones(k)
    levels = np.array([10, -10, 5, -5, 0])
    if k % 512:
        return np.exp2(np.random.permutation(np.resize(levels, k // 32))).repeat(32)
    a = np.empty((k // 512, 16))
    for p in range(k // 512):
        a[p, :8] = np.random.permutation(np.resize(levels, 8))
        for g in range(8):
            far = levels[np.abs(levels - a[p, g]) >= 10]
            a[p, g + 8] = far[np.random.randint(len(far))]
    return np.exp2(a.ravel()).repeat(32)


BF16 = ml_dtypes.bfloat16


def bf(x):
    return np.asarray(x, np.float32).astype(BF16)


def f64(x):
    return np.asarray(x).astype(np.float64)


E2M1 = np.array([0.0, 0.5, 1.0, 1.5, 2.0, 3.0, 4.0, 6.0, -0.0, -0.5, -1.0, -1.5, -2.0, -3.0, -4.0, -6.0])


def pack_weight(w, fmt):
    k, n = w.shape
    w = f64(bf(w)).reshape(k // 32, 32, n)
    amax = np.abs(w).max(1)
    if fmt == "e4m3":
        byte = np.frexp(amax)[1] - 1 + 127 - 7
    else:
        mant, ex = np.frexp(amax / 6.0)
        byte = np.where(mant > 0.5, ex, ex - 1) + 127
    byte = np.clip(np.where(amax > 0, byte, 1), 1, 254)
    scaled = (w * np.exp2(127.0 - byte)[:, None, :]).reshape(k, n).astype(np.float32)
    by_word = np.ascontiguousarray(scaled.reshape(k // 512, 128, 4, n).transpose(0, 1, 3, 2))
    if fmt == "e4m3":
        words = by_word.astype(ml_dtypes.float8_e4m3fn).view(np.uint8)
    else:
        c = by_word.astype(ml_dtypes.float4_e2m1fn).view(np.uint8) & 0xF
        words = c[..., 0::2] | (c[..., 1::2] << 4)
    return np.ascontiguousarray(words), np.ascontiguousarray(byte.astype(np.uint8).reshape(k // 512, 16, n))


def unpack_weight(words, scales, fmt):
    g, p, n, _ = words.shape
    if fmt == "e4m3":
        vals = np.ascontiguousarray(words).view(ml_dtypes.float8_e4m3fn).astype(np.float64)
    else:
        nib = np.empty((g, p, n, 4), np.uint8)
        nib[..., 0::2] = words & 0xF
        nib[..., 1::2] = words >> 4
        vals = E2M1[nib]
    vals = vals * np.repeat(np.exp2(scales.astype(np.float64) - 127.0), 8, axis=1)[..., None]
    return vals.transpose(0, 1, 3, 2).reshape(g * 512, n)
def pack4(w):
    words, scales = pack_weight(w, "e2m1")
    return words.reshape(words.shape[0], 128, -1), scales


def unpack4(words, scales):
    return unpack_weight(words.reshape(words.shape[0], 128, -1, 2), scales, "e2m1")


L, H, B, C, D = 1024, 512, 4, 1024, 1024


def setup_inputs():
    s = mx_kscale(L)
    t = mx_kscale(C)
    lag = np.random.standard_normal((L, H)) / np.sqrt(L) * s[:, None]
    x = np.random.standard_normal((L, B, C)) / s[:, None, None] * t
    w = np.random.standard_normal((C, D)) / np.sqrt(C) / t[:, None]
    lag_words, lag_scales = pack4(lag)
    x_words, x_scales = pack4(x.reshape(L, B * C))
    w_words, w_scales = pack_weight(w, "e4m3")
    return {"lag_words": lag_words, "lag_scales": lag_scales,
            "x_words": x_words, "x_scales": x_scales,
            "w_words": w_words, "w_scales": w_scales,
            "level": bf(0.5 * np.random.standard_normal((B, C)) * t),
            "bias": bf(0.3 * np.random.standard_normal(D))}


def reference(lag_words, lag_scales, x_words, x_scales, w_words, w_scales, level, bias):
    lag = unpack4(lag_words, lag_scales)
    x = unpack4(x_words, x_scales)
    w = unpack_weight(w_words, w_scales, "e4m3")
    m = (lag.T @ x).reshape(H, B, C)
    u = np.maximum(m + f64(level), 0.0)
    u = u.transpose(1, 0, 2).reshape(B * H, C)
    y = (mxq(u, 1, "e4m3") @ w) + f64(bias)
    return y.reshape(B, H, D)

@@ -1,0 +1,265 @@
+from contextlib import ExitStack
+
+import concourse.mybir as mybir
+
+L, H, B, C, D = 1024, 512, 4, 1024, 1024
+FLOPS = 2 * L * H * B * C + 2 * B * H * C * D
+
+F32 = mybir.dt.float32
+BF16 = mybir.dt.bfloat16
+I32 = mybir.dt.int32
+U32 = mybir.dt.uint32
+U8 = mybir.dt.uint8
+FP4X4 = mybir.dt.float4_e2m1fn_x4
+FP8X4 = mybir.dt.float8_e4m3fn_x4
+ADD = mybir.AluOpType.add
+RELU = mybir.ActivationFunctionType.Relu
+
+P = 128
+KG = L // 512
+CG = C // 512
+UNITS = B * CG
+NT = 512
+
+ORDER = """
+W:0.0 S:0 W:0.1 W:0.2 W:0.3 U:0 W:1 S:1 U:1 W:2 S:2 IV:0.512 S:3 IV:1.256 IS:1.256 Q:0 Q:1 W:3 U:2 IS:2.512
+H:0 W:4 SP:0 E:0.0 E:0.1 E:0.2 E:0.3 Q:2 U:3 IS:3.384 H:1 E:1.0 E:1.1 IV:3.128 E:1.2 Q:3 E:1.3 W:5 U:4
+IS:4.512 H:2 W:6 E:2.0 E:2.1 E:2.2 E:2.3 Q:4 U:5 IS:5.384 H:3 E:3.0 E:3.1 IV:5.128 E:3.2 Q:5 E:3.3 W:7 U:6
+IS:6.512 H:4 E:4.0 E:4.1 E:4.2 E:4.3 Q:6 U:7 IS:7.256 H:5 E:5.0 E:5.1 IV:7.256 E:5.2 Q:7 E:5.3 H:6 E:6.0 E:6.1
+E:6.2 E:6.3 H:7 E:7.0 E:7.1 E:7.2 E:7.3
+""".split()
+GROUP_FIRST = (0, 6)
+
+
+def tile_lag_channel_mixer_s4_kernel(
+    tc, lag_words, lag_scales, x_words, x_scales, w_words, w_scales, level, bias, out
+):
+    nc = tc.nc
+    with ExitStack() as ctx:
+        keep = ctx.enter_context(tc.tile_pool(name="keep", bufs=1))
+        work = ctx.enter_context(tc.tile_pool(name="work", bufs=3))
+        outs = ctx.enter_context(tc.tile_pool(name="outs", bufs=6))
+        psum = ctx.enter_context(tc.psum_pool(name="psum", bufs=8))
+        ctx.enter_context(tc.manual_schedule())
+
+        lag_w = keep.tile([P, KG, 2 * H], U8, align_bytes=64, name="lag_w")
+        lag_s = keep.tile([P, KG, H], U8, align_bytes=64, name="lag_s")
+        w_w = keep.tile([P, CG, 4 * D], U8, align_bytes=64, name="w_w")
+        w_s = keep.tile([P, CG, D], U8, align_bytes=64, name="w_s")
+        lvl = keep.tile([P, UNITS, 4], BF16, align_bytes=64, name="lvl")
+        bias_t = keep.tile([P, D], BF16, align_bytes=64, name="bias_t")
+        scratch = keep.tile([P, 1], F32, name="scratch")
+        x_raw = [keep.tile([P, KG, 1024], U8, align_bytes=64, name="x_raw%d" % u) for u in range(UNITS)]
+        x_st = [keep.tile([P, KG, 4, 256], U8, align_bytes=64, name="x_st%d" % u) for u in range(UNITS)]
+        xs_raw0 = keep.tile([P, KG, 2 * C], U8, align_bytes=64, name="xs_raw0")
+        xs_pk = keep.tile([P, 2 * C], U8, align_bytes=64, name="xs_pk")
+        pk_st = keep.tile([P, 2 * CG, 4, P], U8, align_bytes=64, name="pk_st")
+        pl1 = keep.tile([P, 2 * CG, 4, P], U8, align_bytes=64, name="pl1")
+        xs_st = [keep.tile([P, KG, CG, 4, P], U8, align_bytes=64, name="xs_st%d" % b) for b in range(2)]
+        codes = [keep.tile([P, H], U32, align_bytes=64, name="codes%d" % u) for u in range(UNITS)]
+        code_scales = [keep.tile([P, H], U8, align_bytes=64, name="cs%d" % u) for u in range(UNITS)]
+
+        def load_x(u, engine=nc.sync):
+            src = x_words[:, :, u * 1024 : (u + 1) * 1024].bitcast(I32)
+            engine.dma_start(out=x_raw[u][:].bitcast(I32), in_=src.rearrange("k p n -> p k n"))
+
+        def load_scales(engine, dst, src, q):
+            rows = src[:, 4 * q : 4 * q + 4, :].bitcast(I32)
+            engine.dma_start(out=dst[32 * q : 32 * q + 4].bitcast(I32), in_=rows.rearrange("k r n -> r k n"))
+
+        nc.vector.memset(lag_s[:].rearrange("p k n -> p (k n)").bitcast(I32), 0)
+        nc.vector.memset(xs_raw0[:].rearrange("p k n -> p (k n)").bitcast(I32), 0)
+        nc.vector.memset(codes[UNITS - 1][:], 0)
+        nc.vector.memset(code_scales[UNITS - 1][:].bitcast(I32), 0)
+        nc.vector.memset(scratch[:], 0.0)
+        load_x(0)
+        nc.gpsimd.dma_start(out=lag_w[:].bitcast(I32), in_=lag_words[:, :, :].bitcast(I32).rearrange("k p n -> p k n"))
+        for q in range(4):
+            load_scales(nc.scalar if q < 3 else nc.gpsimd, lag_s, lag_scales, q)
+            load_scales(nc.sync, xs_raw0, x_scales[:, :, 0 : 2 * C], q)
+        nc.gpsimd.memset(xs_pk[:].bitcast(I32), 0)
+        nc.gpsimd.memset(pl1[:].rearrange("p a t m -> p (a t m)").bitcast(I32), 0)
+        nc.gpsimd.memset(w_s[:].rearrange("p k n -> p (k n)").bitcast(I32), 0)
+        nc.scalar.activation(out=scratch[:], in_=scratch[:], func=RELU)
+        nc.scalar.dma_start(out=lvl[:], in_=level.rearrange("b (g p t) -> p (b g) t", g=CG, t=4))
+        load_x(1)
+        load_x(2)
+        for q in range(4):
+            nc.sync.dma_start(
+                out=xs_pk[32 * q : 32 * q + 8, :].bitcast(I32),
+                in_=x_scales[:, 4 * q : 4 * q + 4, 2 * C : 4 * C].bitcast(I32),
+            )
+        for q in range(4):
+            load_scales(nc.sync, w_s, w_scales, q)
+        load_x(3)
+        for g in range(CG):
+            nc.sync.dma_start(
+                out=w_w[:, g, :].bitcast(I32),
+                in_=w_words[g].rearrange("p n t -> p (n t)").bitcast(I32),
+            )
+        load_x(4)
+        nc.sync.dma_start(out=bias_t[:], in_=bias.partition_broadcast(P))
+        for u in range(5, UNITS):
+            load_x(u)
+        warm = psum.tile([P, NT], F32, name="acc")
+        for i in range(6):
+            nc.tensor.matmul_mx(
+                out=warm[:],
+                lhsT=codes[UNITS - 1][:, 0:P].bitcast(FP8X4),
+                lhsT_scale=code_scales[UNITS - 1][:, 0:P],
+                rhs=codes[UNITS - 1][:].bitcast(FP8X4),
+                rhs_scale=code_scales[UNITS - 1][:],
+                start=True,
+                stop=True,
+            )
+
+        def words(u):
+            nc.vector.tensor_copy(
+                out=x_st[u][:].rearrange("p k t (m b) -> p k t m b", b=2),
+                in_=x_raw[u][:].rearrange("p k (m t b) -> p k t m b", t=4, b=2),
+            )
+
+        def words_t(u, t):
+            nc.vector.tensor_copy(
+                out=x_st[u][:, :, t, :].rearrange("p k (m b) -> p k m b", b=2),
+                in_=x_raw[u][:].rearrange("p k (m t b) -> p k t m b", t=4, b=2)[:, :, t],
+            )
+
+        def scales(u):
+            b, g = divmod(u, CG)
+            nc.vector.tensor_copy(
+                out=xs_st[b][:, :, g], in_=xs_raw0[:, :, u * 512 : (u + 1) * 512].rearrange("p k (m t) -> p k t m", t=4)
+            )
+
+        def scales_packed():
+            nc.vector.tensor_copy(out=pk_st[:], in_=xs_pk[:].rearrange("p (a m t) -> p a t m", t=4, m=P))
+            for q in range(4):
+                nc.sync.dma_start(
+                    out=pl1[32 * q : 32 * q + 4].bitcast(I32), in_=pk_st[32 * q + 4 : 32 * q + 8].bitcast(I32)
+                )
+
+        def x_scale(u, k, t):
+            if u < 2 * CG:
+                return xs_st[u // CG][:, k, u % CG, t, :]
+            return (pk_st, pl1)[k][:, u - 2 * CG, t, :]
+
+        rows = {}
+        inter = {}
+
+        def stage1(u):
+            rows[u] = work.tile([P, 4, H], BF16, align_bytes=64, name="rows")
+            for t in range(4):
+                acc = psum.tile([P, NT], F32, name="acc")
+                for k in range(KG):
+                    nc.tensor.matmul_mx(
+                        out=acc[:],
+                        lhsT=x_st[u][:, k, t, :].bitcast(FP4X4),
+                        lhsT_scale=x_scale(u, k, t),
+                        rhs=lag_w[:, k, :].bitcast(FP4X4),
+                        rhs_scale=lag_s[:, k, :],
+                        start=(k == 0),
+                        stop=(k == KG - 1),
+                    )
+                nc.scalar.activation(
+                    out=rows[u][:, t, :], in_=acc[:], func=RELU, bias=lvl[:, u, t : t + 1]
+                )
+
+        def get_inter(u):
+            if u not in inter:
+                inter[u] = work.tile([P, H, 4], BF16, align_bytes=64, name="inter")
+            return inter[u]
+
+        filled = {}
+
+        def interleave(engine_copy, u, n):
+            n0 = filled.get(u, 0)
+            filled[u] = n0 + n
+            engine_copy(
+                out=get_inter(u)[:, n0 : n0 + n, :].rearrange("p (c i) t -> p c t i", i=4),
+                in_=rows[u][:, :, n0 : n0 + n].rearrange("p t (c i) -> p c t i", i=4),
+            )
+
+        def interleave_g(out, in_):
+            nc.gpsimd.tensor_scalar(out=out, in0=in_, scalar1=1.0, scalar2=0.0, op0=mybir.AluOpType.mult, op1=ADD)
+
+        def quantise(u):
+            nc.vector.quantize_mx(
+                out=codes[u][:].bitcast(FP8X4),
+                scales=code_scales[u][:],
+                in_=inter[u][:].rearrange("p n t -> p (n t)"),
+            )
+
+        y_tiles = {}
+        banks = {}
+
+        def multiply(j, i, g, start, stop):
+            u = (j // 2) * CG + g
+            m, d = 2 * (j % 2) + i // 2, i % 2
+            if start:
+                banks[j, i] = psum.tile([P, NT], F32, name="acc")
+            nc.tensor.matmul_mx(
+                out=banks[j, i][:],
+                lhsT=codes[u][:, m * P : (m + 1) * P].bitcast(FP8X4),
+                lhsT_scale=code_scales[u][:, m * P : (m + 1) * P],
+                rhs=w_w[:, g, 4 * d * NT : 4 * (d + 1) * NT].bitcast(FP8X4),
+                rhs_scale=w_s[:, g, d * NT : (d + 1) * NT],
+                start=start,
+                stop=stop,
+            )
+
+        def stage2(j):
+            if j in GROUP_FIRST:
+                for g in range(CG):
+                    for i in range(4):
+                        multiply(j, i, g, g == 0, g == CG - 1)
+            else:
+                for i in range(4):
+                    for g in range(CG):
+                        multiply(j, i, g, g == 0, g == CG - 1)
+
+        def finish(j, i):
+            b, m, d = j // 2, 2 * (j % 2) + i // 2, i % 2
+            if d == 0:
+                y_tiles[b, m] = outs.tile([P, D], F32, name="y")
+            y = y_tiles[b, m]
+            acc = banks[j, i]
+            rows_out = out[b, m * P : (m + 1) * P, :]
+            pieces = 2 if (j, i) == (7, 3) else 1
+            width = NT // pieces
+            for c in range(pieces):
+                cols = slice(d * NT + c * width, d * NT + (c + 1) * width)
+                nc.vector.tensor_tensor(
+                    out=y[:, cols], in0=acc[:, c * width : (c + 1) * width], in1=bias_t[:, cols], op=ADD
+                )
+                if j == 7:
+                    engine = nc.scalar if (i + c) % 2 else nc.sync
+                    engine.dma_start(out=rows_out[:, cols], in_=y[:, cols])
+            if j < 7 and d == D // NT - 1:
+                nc.sync.dma_start(out=rows_out, in_=y[:])
+
+        for token in ORDER:
+            kind, rest = token.split(":")
+            a = [int(v) for v in rest.split(".")]
+            if kind == "W":
+                if len(a) == 1:
+                    words(a[0])
+                else:
+                    words_t(a[0], a[1])
+            elif kind == "S":
+                scales(a[0])
+            elif kind == "SP":
+                scales_packed()
+            elif kind == "U":
+                stage1(a[0])
+            elif kind == "IV":
+                interleave(nc.vector.tensor_copy, a[0], a[1])
+            elif kind == "IS":
+                interleave(nc.scalar.copy, a[0], a[1])
+            elif kind == "IG":
+                interleave(interleave_g, a[0], a[1])
+            elif kind == "Q":
+                quantise(a[0])
+            elif kind == "H":
+                stage2(a[0])
+            elif kind == "E":
+                finish(a[0], a[1])

@@ -9,6 +9,7 @@ F32 = mybir.dt.float32
 BF16 = mybir.dt.bfloat16
 I32 = mybir.dt.int32
 U32 = mybir.dt.uint32
+U16 = mybir.dt.uint16
 U8 = mybir.dt.uint8
 FP4X4 = mybir.dt.float4_e2m1fn_x4
 FP8X4 = mybir.dt.float8_e4m3fn_x4
@@ -20,15 +21,9 @@ KG = L // 512
 CG = C // 512
 UNITS = B * CG
 NT = 512
-
-ORDER = """
-W:0.0 S:0 W:0.1 W:0.2 W:0.3 U:0 W:1 S:1 U:1 W:2 S:2 IV:0.512 S:3 IV:1.256 IS:1.256 Q:0 Q:1 W:3 U:2 IS:2.512
-H:0 W:4 SP:0 E:0.0 E:0.1 E:0.2 E:0.3 Q:2 U:3 IS:3.384 H:1 E:1.0 E:1.1 IV:3.128 E:1.2 Q:3 E:1.3 W:5 U:4
-IS:4.512 H:2 W:6 E:2.0 E:2.1 E:2.2 E:2.3 Q:4 U:5 IS:5.384 H:3 E:3.0 E:3.1 IV:5.128 E:3.2 Q:5 E:3.3 W:7 U:6
-IS:6.512 H:4 E:4.0 E:4.1 E:4.2 E:4.3 Q:6 U:7 IS:7.256 H:5 E:5.0 E:5.1 IV:7.256 E:5.2 Q:7 E:5.3 H:6 E:6.0 E:6.1
-E:6.2 E:6.3 H:7 E:7.0 E:7.1 E:7.2 E:7.3
-""".split()
-GROUP_FIRST = (0, 6)
+HALF = H // 2
+X_LOADS = ((0, 1), (1, 1), (2, 2), (4, 4))
+V_SHARE = 128
 
 
 def tile_lag_channel_mixer_s4_kernel(
@@ -38,110 +33,73 @@ def tile_lag_channel_mixer_s4_kernel(
     with ExitStack() as ctx:
         keep = ctx.enter_context(tc.tile_pool(name="keep", bufs=1))
         work = ctx.enter_context(tc.tile_pool(name="work", bufs=3))
-        outs = ctx.enter_context(tc.tile_pool(name="outs", bufs=6))
+        outs = ctx.enter_context(tc.tile_pool(name="outs", bufs=8))
         psum = ctx.enter_context(tc.psum_pool(name="psum", bufs=8))
         ctx.enter_context(tc.manual_schedule())
 
         lag_w = keep.tile([P, KG, 2 * H], U8, align_bytes=64, name="lag_w")
         lag_s = keep.tile([P, KG, H], U8, align_bytes=64, name="lag_s")
         w_w = keep.tile([P, CG, 4 * D], U8, align_bytes=64, name="w_w")
-        w_s = keep.tile([P, CG, D], U8, align_bytes=64, name="w_s")
+        w_s = keep.tile([P, D], U8, align_bytes=64, name="w_s")
         lvl = keep.tile([P, UNITS, 4], BF16, align_bytes=64, name="lvl")
         bias_t = keep.tile([P, D], BF16, align_bytes=64, name="bias_t")
-        scratch = keep.tile([P, 1], F32, name="scratch")
-        x_raw = [keep.tile([P, KG, 1024], U8, align_bytes=64, name="x_raw%d" % u) for u in range(UNITS)]
+        x_raw = {u0: keep.tile([P, KG, n * 1024], U8, align_bytes=64, name="x_raw%d" % u0) for u0, n in X_LOADS}
         x_st = [keep.tile([P, KG, 4, 256], U8, align_bytes=64, name="x_st%d" % u) for u in range(UNITS)]
-        xs_raw0 = keep.tile([P, KG, 2 * C], U8, align_bytes=64, name="xs_raw0")
-        xs_pk = keep.tile([P, 2 * C], U8, align_bytes=64, name="xs_pk")
-        pk_st = keep.tile([P, 2 * CG, 4, P], U8, align_bytes=64, name="pk_st")
-        pl1 = keep.tile([P, 2 * CG, 4, P], U8, align_bytes=64, name="pl1")
-        xs_st = [keep.tile([P, KG, CG, 4, P], U8, align_bytes=64, name="xs_st%d" % b) for b in range(2)]
+        xs_first = keep.tile([P, KG, C], U8, align_bytes=64, name="xs_first")
+        xs_rest = keep.tile([P, KG, (B - 1) * C], U8, align_bytes=64, name="xs_rest")
+        xs_st = [keep.tile([P, KG, 4, P], U8, align_bytes=64, name="xs_st%d" % u) for u in range(UNITS)]
         codes = [keep.tile([P, H], U32, align_bytes=64, name="codes%d" % u) for u in range(UNITS)]
         code_scales = [keep.tile([P, H], U8, align_bytes=64, name="cs%d" % u) for u in range(UNITS)]
 
-        def load_x(u, engine=nc.sync):
-            src = x_words[:, :, u * 1024 : (u + 1) * 1024].bitcast(I32)
-            engine.dma_start(out=x_raw[u][:].bitcast(I32), in_=src.rearrange("k p n -> p k n"))
+        def load_x(index):
+            u0, n = X_LOADS[index]
+            src = x_words[:, :, u0 * 1024 : (u0 + n) * 1024].bitcast(I32)
+            nc.sync.dma_start(out=x_raw[u0][:].bitcast(I32), in_=src.rearrange("k p n -> p k n"))
 
         def load_scales(engine, dst, src, q):
             rows = src[:, 4 * q : 4 * q + 4, :].bitcast(I32)
             engine.dma_start(out=dst[32 * q : 32 * q + 4].bitcast(I32), in_=rows.rearrange("k r n -> r k n"))
 
-        nc.vector.memset(lag_s[:].rearrange("p k n -> p (k n)").bitcast(I32), 0)
-        nc.vector.memset(xs_raw0[:].rearrange("p k n -> p (k n)").bitcast(I32), 0)
-        nc.vector.memset(codes[UNITS - 1][:], 0)
-        nc.vector.memset(code_scales[UNITS - 1][:].bitcast(I32), 0)
-        nc.vector.memset(scratch[:], 0.0)
+        def zero(tile):
+            nc.vector.memset(tile.bitcast(I32), 0)
+
+        zero(xs_first[:].rearrange("p k n -> p (k n)"))
+        zero(lag_s[:].rearrange("p k n -> p (k n)"))
+        zero(xs_rest[:].rearrange("p k n -> p (k n)"))
+        zero(w_s[:])
         load_x(0)
-        nc.gpsimd.dma_start(out=lag_w[:].bitcast(I32), in_=lag_words[:, :, :].bitcast(I32).rearrange("k p n -> p k n"))
+        nc.scalar.dma_start(out=lag_w[:].bitcast(I32), in_=lag_words[:, :, :].bitcast(I32).rearrange("k p n -> p k n"))
         for q in range(4):
-            load_scales(nc.scalar if q < 3 else nc.gpsimd, lag_s, lag_scales, q)
-            load_scales(nc.sync, xs_raw0, x_scales[:, :, 0 : 2 * C], q)
-        nc.gpsimd.memset(xs_pk[:].bitcast(I32), 0)
-        nc.gpsimd.memset(pl1[:].rearrange("p a t m -> p (a t m)").bitcast(I32), 0)
-        nc.gpsimd.memset(w_s[:].rearrange("p k n -> p (k n)").bitcast(I32), 0)
-        nc.scalar.activation(out=scratch[:], in_=scratch[:], func=RELU)
+            load_scales(nc.sync, xs_first, x_scales[:, :, 0:C], q)
+            load_scales(nc.scalar, lag_s, lag_scales, q)
         nc.scalar.dma_start(out=lvl[:], in_=level.rearrange("b (g p t) -> p (b g) t", g=CG, t=4))
         load_x(1)
         load_x(2)
         for q in range(4):
-            nc.sync.dma_start(
-                out=xs_pk[32 * q : 32 * q + 8, :].bitcast(I32),
-                in_=x_scales[:, 4 * q : 4 * q + 4, 2 * C : 4 * C].bitcast(I32),
-            )
+            load_scales(nc.sync, xs_rest, x_scales[:, :, C : B * C], q)
         for q in range(4):
-            load_scales(nc.sync, w_s, w_scales, q)
-        load_x(3)
-        for g in range(CG):
             nc.sync.dma_start(
-                out=w_w[:, g, :].bitcast(I32),
-                in_=w_words[g].rearrange("p n t -> p (n t)").bitcast(I32),
+                out=w_s[32 * q : 32 * q + 4 * CG, :].bitcast(I32),
+                in_=w_scales[:, 4 * q : 4 * q + 4, :].bitcast(I32),
             )
-        load_x(4)
+        nc.sync.dma_start(out=w_w[:].bitcast(I32), in_=w_words.rearrange("g p n t -> p g (n t)").bitcast(I32))
         nc.sync.dma_start(out=bias_t[:], in_=bias.partition_broadcast(P))
-        for u in range(5, UNITS):
-            load_x(u)
-        warm = psum.tile([P, NT], F32, name="acc")
-        for i in range(6):
-            nc.tensor.matmul_mx(
-                out=warm[:],
-                lhsT=codes[UNITS - 1][:, 0:P].bitcast(FP8X4),
-                lhsT_scale=code_scales[UNITS - 1][:, 0:P],
-                rhs=codes[UNITS - 1][:].bitcast(FP8X4),
-                rhs_scale=code_scales[UNITS - 1][:],
-                start=True,
-                stop=True,
-            )
+        load_x(3)
 
-        def words(u):
+        def regroup_words(u):
+            u0 = max(first for first, n in X_LOADS if first <= u)
             nc.vector.tensor_copy(
-                out=x_st[u][:].rearrange("p k t (m b) -> p k t m b", b=2),
-                in_=x_raw[u][:].rearrange("p k (m t b) -> p k t m b", t=4, b=2),
+                out=x_st[u][:].bitcast(U16),
+                in_=x_raw[u0][:, :, (u - u0) * 1024 : (u - u0 + 1) * 1024].bitcast(U16).rearrange("p k (m t) -> p k t m", t=4),
             )
 
-        def words_t(u, t):
-            nc.vector.tensor_copy(
-                out=x_st[u][:, :, t, :].rearrange("p k (m b) -> p k m b", b=2),
-                in_=x_raw[u][:].rearrange("p k (m t b) -> p k t m b", t=4, b=2)[:, :, t],
-            )
+        def regroup_scales(u, t0=0, t1=4):
+            raw = xs_first[:, :, u * 512 : (u + 1) * 512] if u < CG else xs_rest[:, :, (u - CG) * 512 : (u - CG + 1) * 512]
+            nc.vector.tensor_copy(out=xs_st[u][:, :, t0:t1], in_=raw.rearrange("p k (m t) -> p k t m", t=4)[:, :, t0:t1])
 
-        def scales(u):
-            b, g = divmod(u, CG)
-            nc.vector.tensor_copy(
-                out=xs_st[b][:, :, g], in_=xs_raw0[:, :, u * 512 : (u + 1) * 512].rearrange("p k (m t) -> p k t m", t=4)
-            )
-
-        def scales_packed():
-            nc.vector.tensor_copy(out=pk_st[:], in_=xs_pk[:].rearrange("p (a m t) -> p a t m", t=4, m=P))
-            for q in range(4):
-                nc.sync.dma_start(
-                    out=pl1[32 * q : 32 * q + 4].bitcast(I32), in_=pk_st[32 * q + 4 : 32 * q + 8].bitcast(I32)
-                )
-
-        def x_scale(u, k, t):
-            if u < 2 * CG:
-                return xs_st[u // CG][:, k, u % CG, t, :]
-            return (pk_st, pl1)[k][:, u - 2 * CG, t, :]
+        def regroup(u):
+            regroup_words(u)
+            regroup_scales(u)
 
         rows = {}
         inter = {}
@@ -154,112 +112,122 @@ def tile_lag_channel_mixer_s4_kernel(
                     nc.tensor.matmul_mx(
                         out=acc[:],
                         lhsT=x_st[u][:, k, t, :].bitcast(FP4X4),
-                        lhsT_scale=x_scale(u, k, t),
+                        lhsT_scale=xs_st[u][:, k, t, :],
                         rhs=lag_w[:, k, :].bitcast(FP4X4),
                         rhs_scale=lag_s[:, k, :],
                         start=(k == 0),
                         stop=(k == KG - 1),
                     )
-                nc.scalar.activation(
-                    out=rows[u][:, t, :], in_=acc[:], func=RELU, bias=lvl[:, u, t : t + 1]
-                )
+                nc.scalar.activation(out=rows[u][:, t, :], in_=acc[:], func=RELU, bias=lvl[:, u, t : t + 1])
 
-        def get_inter(u):
+        def interleave(copy, u, n0, n1):
             if u not in inter:
                 inter[u] = work.tile([P, H, 4], BF16, align_bytes=64, name="inter")
-            return inter[u]
-
-        filled = {}
-
-        def interleave(engine_copy, u, n):
-            n0 = filled.get(u, 0)
-            filled[u] = n0 + n
-            engine_copy(
-                out=get_inter(u)[:, n0 : n0 + n, :].rearrange("p (c i) t -> p c t i", i=4),
-                in_=rows[u][:, :, n0 : n0 + n].rearrange("p t (c i) -> p c t i", i=4),
+            copy(
+                out=inter[u][:, n0:n1, :].rearrange("p (c i) t -> p c t i", i=4),
+                in_=rows[u][:, :, n0:n1].rearrange("p t (c i) -> p c t i", i=4),
             )
 
-        def interleave_g(out, in_):
-            nc.gpsimd.tensor_scalar(out=out, in0=in_, scalar1=1.0, scalar2=0.0, op0=mybir.AluOpType.mult, op1=ADD)
-
-        def quantise(u):
+        def quantise(u, half):
+            cols = slice(half * HALF, (half + 1) * HALF)
             nc.vector.quantize_mx(
-                out=codes[u][:].bitcast(FP8X4),
-                scales=code_scales[u][:],
-                in_=inter[u][:].rearrange("p n t -> p (n t)"),
+                out=codes[u][:, cols].bitcast(FP8X4),
+                scales=code_scales[u][:, cols],
+                in_=inter[u][:, cols, :].rearrange("p n t -> p (n t)"),
             )
 
-        y_tiles = {}
         banks = {}
+        y_tiles = {}
 
-        def multiply(j, i, g, start, stop):
+        def multiply(j, i, g):
             u = (j // 2) * CG + g
             m, d = 2 * (j % 2) + i // 2, i % 2
-            if start:
+            if g == 0:
                 banks[j, i] = psum.tile([P, NT], F32, name="acc")
             nc.tensor.matmul_mx(
                 out=banks[j, i][:],
                 lhsT=codes[u][:, m * P : (m + 1) * P].bitcast(FP8X4),
                 lhsT_scale=code_scales[u][:, m * P : (m + 1) * P],
                 rhs=w_w[:, g, 4 * d * NT : 4 * (d + 1) * NT].bitcast(FP8X4),
-                rhs_scale=w_s[:, g, d * NT : (d + 1) * NT],
-                start=start,
-                stop=stop,
+                rhs_scale=w_s[4 * g : P, d * NT : (d + 1) * NT],
+                start=(g == 0),
+                stop=(g == CG - 1),
             )
 
-        def stage2(j):
-            if j in GROUP_FIRST:
+        def stage2(j, group_first=False):
+            if group_first:
                 for g in range(CG):
                     for i in range(4):
-                        multiply(j, i, g, g == 0, g == CG - 1)
+                        multiply(j, i, g)
             else:
                 for i in range(4):
                     for g in range(CG):
-                        multiply(j, i, g, g == 0, g == CG - 1)
+                        multiply(j, i, g)
 
-        def finish(j, i):
+        def finish(j, i, pieces=1):
             b, m, d = j // 2, 2 * (j % 2) + i // 2, i % 2
             if d == 0:
                 y_tiles[b, m] = outs.tile([P, D], F32, name="y")
             y = y_tiles[b, m]
-            acc = banks[j, i]
             rows_out = out[b, m * P : (m + 1) * P, :]
-            pieces = 2 if (j, i) == (7, 3) else 1
             width = NT // pieces
+            last = j == UNITS - 1
             for c in range(pieces):
                 cols = slice(d * NT + c * width, d * NT + (c + 1) * width)
                 nc.vector.tensor_tensor(
-                    out=y[:, cols], in0=acc[:, c * width : (c + 1) * width], in1=bias_t[:, cols], op=ADD
+                    out=y[:, cols], in0=banks[j, i][:, c * width : (c + 1) * width], in1=bias_t[:, cols], op=ADD
                 )
-                if j == 7:
+                if last:
                     engine = nc.scalar if (i + c) % 2 else nc.sync
                     engine.dma_start(out=rows_out[:, cols], in_=y[:, cols])
-            if j < 7 and d == D // NT - 1:
+            if not last and d == D // NT - 1:
                 nc.sync.dma_start(out=rows_out, in_=y[:])
 
-        for token in ORDER:
-            kind, rest = token.split(":")
-            a = [int(v) for v in rest.split(".")]
-            if kind == "W":
-                if len(a) == 1:
-                    words(a[0])
-                else:
-                    words_t(a[0], a[1])
-            elif kind == "S":
-                scales(a[0])
-            elif kind == "SP":
-                scales_packed()
-            elif kind == "U":
-                stage1(a[0])
-            elif kind == "IV":
-                interleave(nc.vector.tensor_copy, a[0], a[1])
-            elif kind == "IS":
-                interleave(nc.scalar.copy, a[0], a[1])
-            elif kind == "IG":
-                interleave(interleave_g, a[0], a[1])
-            elif kind == "Q":
-                quantise(a[0])
-            elif kind == "H":
-                stage2(a[0])
-            elif kind == "E":
-                finish(a[0], a[1])
+        vcopy, scopy = nc.vector.tensor_copy, nc.scalar.copy
+
+        regroup_words(0)
+        regroup_scales(0, 0, 1)
+        regroup_scales(0, 1, 4)
+        stage1(0)
+        regroup(1)
+        stage1(1)
+        regroup(2)
+        regroup_words(3)
+        interleave(vcopy, 0, 0, H)
+        regroup_scales(3)
+        quantise(0, 0)
+        quantise(0, 1)
+        stage1(2)
+        interleave(vcopy, 1, 0, HALF)
+        regroup_scales(4)
+        quantise(1, 0)
+        interleave(vcopy, 1, HALF, H)
+        regroup_words(4)
+        quantise(1, 1)
+        stage2(0, group_first=True)
+        interleave(scopy, 2, 0, HALF)
+        interleave(scopy, 2, HALF, H)
+        for u in range(3, UNITS):
+            stage1(u)
+            for i in range(4):
+                finish(u - 3, i)
+            if u > 3:
+                interleave(vcopy, u - 1, H - V_SHARE, H)
+            quantise(u - 1, 0)
+            if u + 2 < UNITS:
+                regroup(u + 2)
+            quantise(u - 1, 1)
+            stage2(u - 2)
+            interleave(scopy, u, 0, HALF)
+            interleave(scopy, u, HALF, H - V_SHARE if u < UNITS - 1 else H)
+        finish(5, 0)
+        finish(5, 1)
+        quantise(7, 0)
+        stage2(6)
+        finish(5, 2)
+        finish(5, 3)
+        quantise(7, 1)
+        stage2(7)
+        for j in (6, 7):
+            for i in range(4):
+                finish(j, i, 2 if (j, i) == (7, 3) else 1)

@@ -1,6 +1,7 @@
 from contextlib import ExitStack
 
 import concourse.mybir as mybir
+from concourse.masks import make_identity
 
 L, H, B, C, D = 1024, 512, 4, 1024, 1024
 FLOPS = 2 * L * H * B * C + 2 * B * H * C * D
@@ -22,7 +23,8 @@ CG = C // 512
 UNITS = B * CG
 NT = 512
 HALF = H // 2
-X_LOADS = ((0, 1), (1, 1), (2, 2), (4, 4))
+X_LOADS = ((0, 1), (1, 2), (3, 1), (4, 4))
+XS_LOADS = ((0, 2), (2, 2), (4, 4))
 V_SHARE = 128
 
 
@@ -41,12 +43,14 @@ def tile_lag_channel_mixer_s4_kernel(
         lag_s = keep.tile([P, KG, H], U8, align_bytes=64, name="lag_s")
         w_w = keep.tile([P, CG, 4 * D], U8, align_bytes=64, name="w_w")
         w_s = keep.tile([P, D], U8, align_bytes=64, name="w_s")
-        lvl = keep.tile([P, UNITS, 4], BF16, align_bytes=64, name="lvl")
+        lvl = keep.tile([P, 4, UNITS], F32, align_bytes=64, name="lvl")
+        level_rows = keep.tile([P, 512], BF16, align_bytes=64, name="level_rows")
+        bias_cols = keep.tile([P, D // NT, 4], BF16, align_bytes=64, name="bias_cols")
+        ident = keep.tile([P, P], BF16, align_bytes=64, name="ident")
         bias_t = keep.tile([P, D], BF16, align_bytes=64, name="bias_t")
         x_raw = {u0: keep.tile([P, KG, n * 1024], U8, align_bytes=64, name="x_raw%d" % u0) for u0, n in X_LOADS}
         x_st = [keep.tile([P, KG, 4, 256], U8, align_bytes=64, name="x_st%d" % u) for u in range(UNITS)]
-        xs_first = keep.tile([P, KG, C], U8, align_bytes=64, name="xs_first")
-        xs_rest = keep.tile([P, KG, (B - 1) * C], U8, align_bytes=64, name="xs_rest")
+        xs_raw = {u0: keep.tile([P, KG, n * 512], U8, align_bytes=64, name="xs_raw%d" % u0) for u0, n in XS_LOADS}
         xs_st = [keep.tile([P, KG, 4, P], U8, align_bytes=64, name="xs_st%d" % u) for u in range(UNITS)]
         codes = [keep.tile([P, H], U32, align_bytes=64, name="codes%d" % u) for u in range(UNITS)]
         code_scales = [keep.tile([P, H], U8, align_bytes=64, name="cs%d" % u) for u in range(UNITS)]
@@ -63,28 +67,46 @@ def tile_lag_channel_mixer_s4_kernel(
         def zero(tile):
             nc.vector.memset(tile.bitcast(I32), 0)
 
-        zero(xs_first[:].rearrange("p k n -> p (k n)"))
+        def load_x_scales(index):
+            u0, n = XS_LOADS[index]
+            for q in range(4):
+                load_scales(nc.sync, xs_raw[u0], x_scales[:, :, u0 * 512 : (u0 + n) * 512], q)
+
+        zero(xs_raw[0][:].rearrange("p k n -> p (k n)"))
         zero(lag_s[:].rearrange("p k n -> p (k n)"))
-        zero(xs_rest[:].rearrange("p k n -> p (k n)"))
+        zero(xs_raw[2][:].rearrange("p k n -> p (k n)"))
         zero(w_s[:])
+        nc.scalar.dma_start(out=bias_cols[:], in_=bias.rearrange("(d p c) -> p d c", p=P, c=4))
+        nc.gpsimd.memset(level_rows[:].bitcast(I32), 0)
+        nc.gpsimd.dma_start(out=level_rows[0:UNITS, :], in_=level.rearrange("b (g n) -> (b g) n", g=CG))
+        make_identity(nc, ident[:])
         load_x(0)
         nc.scalar.dma_start(out=lag_w[:].bitcast(I32), in_=lag_words[:, :, :].bitcast(I32).rearrange("k p n -> p k n"))
+        load_x_scales(0)
         for q in range(4):
-            load_scales(nc.sync, xs_first, x_scales[:, :, 0:C], q)
             load_scales(nc.scalar, lag_s, lag_scales, q)
-        nc.scalar.dma_start(out=lvl[:], in_=level.rearrange("b (g p t) -> p (b g) t", g=CG, t=4))
         load_x(1)
-        load_x(2)
-        for q in range(4):
-            load_scales(nc.sync, xs_rest, x_scales[:, :, C : B * C], q)
+        load_x_scales(1)
         for q in range(4):
             nc.sync.dma_start(
                 out=w_s[32 * q : 32 * q + 4 * CG, :].bitcast(I32),
                 in_=w_scales[:, 4 * q : 4 * q + 4, :].bitcast(I32),
             )
         nc.sync.dma_start(out=w_w[:].bitcast(I32), in_=w_words.rearrange("g p n t -> p g (n t)").bitcast(I32))
-        nc.sync.dma_start(out=bias_t[:], in_=bias.partition_broadcast(P))
-        load_x(3)
+        load_x(2)
+
+        bias_bank = psum.tile([P, D // NT, 4, P], BF16, name="acc")
+        for d in range(D // NT):
+            for c in range(4):
+                nc.tensor.transpose(bias_bank[:, d, c, :], bias_cols[:, d, c : c + 1].to_broadcast([P, P]), ident[:])
+        level_bank = psum.tile([P, 4, P], BF16, name="acc")
+        for t in range(4):
+            nc.tensor.transpose(level_bank[:, t, :], level_rows[:, t:512:4], ident[:])
+        nc.scalar.copy(
+            out=bias_t[:].rearrange("p (d n c) -> p d n c", d=D // NT, c=4),
+            in_=bias_bank[:].rearrange("p d c n -> p d n c"),
+        )
+        nc.scalar.copy(out=lvl[:], in_=level_bank[:, :, 0:UNITS])
 
         def regroup_words(u):
             u0 = max(first for first, n in X_LOADS if first <= u)
@@ -94,7 +116,8 @@ def tile_lag_channel_mixer_s4_kernel(
             )
 
         def regroup_scales(u, t0=0, t1=4):
-            raw = xs_first[:, :, u * 512 : (u + 1) * 512] if u < CG else xs_rest[:, :, (u - CG) * 512 : (u - CG + 1) * 512]
+            u0 = max(first for first, n in XS_LOADS if first <= u)
+            raw = xs_raw[u0][:, :, (u - u0) * 512 : (u - u0 + 1) * 512]
             nc.vector.tensor_copy(out=xs_st[u][:, :, t0:t1], in_=raw.rearrange("p k (m t) -> p k t m", t=4)[:, :, t0:t1])
 
         def regroup(u):
@@ -118,7 +141,7 @@ def tile_lag_channel_mixer_s4_kernel(
                         start=(k == 0),
                         stop=(k == KG - 1),
                     )
-                nc.scalar.activation(out=rows[u][:, t, :], in_=acc[:], func=RELU, bias=lvl[:, u, t : t + 1])
+                nc.scalar.activation(out=rows[u][:, t, :], in_=acc[:], func=RELU, bias=lvl[:, t, u : u + 1])
 
         def interleave(copy, u, n0, n1):
             if u not in inter:
@@ -190,20 +213,22 @@ def tile_lag_channel_mixer_s4_kernel(
         regroup_scales(0, 1, 4)
         stage1(0)
         regroup(1)
+        zero(xs_raw[4][:].rearrange("p k n -> p (k n)"))
+        load_x_scales(2)
+        load_x(3)
         stage1(1)
-        regroup(2)
-        regroup_words(3)
+        regroup_words(2)
         interleave(vcopy, 0, 0, H)
-        regroup_scales(3)
+        regroup_scales(2)
         quantise(0, 0)
         quantise(0, 1)
         stage1(2)
         interleave(vcopy, 1, 0, HALF)
-        regroup_scales(4)
-        quantise(1, 0)
         interleave(vcopy, 1, HALF, H)
-        regroup_words(4)
+        quantise(1, 0)
+        regroup_scales(3)
         quantise(1, 1)
+        regroup_words(3)
         stage2(0, group_first=True)
         interleave(scopy, 2, 0, HALF)
         interleave(scopy, 2, HALF, H)
@@ -214,8 +239,8 @@ def tile_lag_channel_mixer_s4_kernel(
             if u > 3:
                 interleave(vcopy, u - 1, H - V_SHARE, H)
             quantise(u - 1, 0)
-            if u + 2 < UNITS:
-                regroup(u + 2)
+            if u + 1 < UNITS:
+                regroup(u + 1)
             quantise(u - 1, 1)
             stage2(u - 2)
             interleave(scopy, u, 0, HALF)

@@ -24,8 +24,10 @@ UNITS = B * CG
 NT = 512
 HALF = H // 2
 X_LOADS = ((0, 1), (1, 2), (3, 1), (4, 4))
-XS_LOADS = ((0, 2), (2, 2), (4, 4))
-V_SHARE = 128
+XS_LOADS = ((0, 2), (2, 2))
+PACKED = 4
+V_SHARE = 192
+BY_SCALAR = ((6, 1), (6, 3))
 
 
 def tile_lag_channel_mixer_s4_kernel(
@@ -51,7 +53,10 @@ def tile_lag_channel_mixer_s4_kernel(
         x_raw = {u0: keep.tile([P, KG, n * 1024], U8, align_bytes=64, name="x_raw%d" % u0) for u0, n in X_LOADS}
         x_st = [keep.tile([P, KG, 4, 256], U8, align_bytes=64, name="x_st%d" % u) for u in range(UNITS)]
         xs_raw = {u0: keep.tile([P, KG, n * 512], U8, align_bytes=64, name="xs_raw%d" % u0) for u0, n in XS_LOADS}
-        xs_st = [keep.tile([P, KG, 4, P], U8, align_bytes=64, name="xs_st%d" % u) for u in range(UNITS)]
+        xs_st = [keep.tile([P, KG, 4, P], U8, align_bytes=64, name="xs_st%d" % u) for u in range(PACKED)]
+        pk_raw = keep.tile([P, 512], U8, align_bytes=64, name="pk_raw")
+        pk_st = keep.tile([P, 4, P], U8, align_bytes=64, name="pk_st")
+        xs_late = keep.tile([P, UNITS - PACKED, KG, 4, P], U8, align_bytes=64, name="xs_late")
         codes = [keep.tile([P, H], U32, align_bytes=64, name="codes%d" % u) for u in range(UNITS)]
         code_scales = [keep.tile([P, H], U8, align_bytes=64, name="cs%d" % u) for u in range(UNITS)]
 
@@ -87,6 +92,9 @@ def tile_lag_channel_mixer_s4_kernel(
             load_scales(nc.scalar, lag_s, lag_scales, q)
         load_x(1)
         load_x_scales(1)
+        for k in range(KG):
+            rows_k = x_scales[k, :, PACKED * 512 : UNITS * 512].bitcast(I32)
+            nc.sync.dma_start(out=pk_raw[k:P:KG, :].bitcast(I32), in_=rows_k.rearrange("q (u n) -> q u n", n=P))
         for q in range(4):
             nc.sync.dma_start(
                 out=w_s[32 * q : 32 * q + 4 * CG, :].bitcast(I32),
@@ -94,6 +102,7 @@ def tile_lag_channel_mixer_s4_kernel(
             )
         nc.sync.dma_start(out=w_w[:].bitcast(I32), in_=w_words.rearrange("g p n t -> p g (n t)").bitcast(I32))
         load_x(2)
+        load_x(3)
 
         bias_bank = psum.tile([P, D // NT, 4, P], BF16, name="acc")
         for d in range(D // NT):
@@ -124,6 +133,17 @@ def tile_lag_channel_mixer_s4_kernel(
             regroup_words(u)
             regroup_scales(u)
 
+        def regroup_packed_scales():
+            nc.vector.tensor_copy(out=pk_st[:], in_=pk_raw[:].rearrange("p (m t) -> p t m", t=4))
+            for q in range(4):
+                nc.sync.dma_start(
+                    out=xs_late[32 * q : 32 * q + 4].rearrange("p u k t m -> p (u k) (t m)").bitcast(I32),
+                    in_=pk_st[32 * q : 32 * q + 32].rearrange("p t m -> p (t m)").bitcast(I32),
+                )
+
+        def x_scale(u, k, t):
+            return xs_st[u][:, k, t, :] if u < PACKED else xs_late[:, u - PACKED, k, t, :]
+
         rows = {}
         inter = {}
 
@@ -135,7 +155,7 @@ def tile_lag_channel_mixer_s4_kernel(
                     nc.tensor.matmul_mx(
                         out=acc[:],
                         lhsT=x_st[u][:, k, t, :].bitcast(FP4X4),
-                        lhsT_scale=xs_st[u][:, k, t, :],
+                        lhsT_scale=x_scale(u, k, t),
                         rhs=lag_w[:, k, :].bitcast(FP4X4),
                         rhs_scale=lag_s[:, k, :],
                         start=(k == 0),
@@ -151,8 +171,8 @@ def tile_lag_channel_mixer_s4_kernel(
                 in_=rows[u][:, :, n0:n1].rearrange("p t (c i) -> p c t i", i=4),
             )
 
-        def quantise(u, half):
-            cols = slice(half * HALF, (half + 1) * HALF)
+        def quantise(u, part, width=HALF):
+            cols = slice(part * width, (part + 1) * width)
             nc.vector.quantize_mx(
                 out=codes[u][:, cols].bitcast(FP8X4),
                 scales=code_scales[u][:, cols],
@@ -161,6 +181,7 @@ def tile_lag_channel_mixer_s4_kernel(
 
         banks = {}
         y_tiles = {}
+        late = []
 
         def multiply(j, i, g):
             u = (j // 2) * CG + g
@@ -194,15 +215,20 @@ def tile_lag_channel_mixer_s4_kernel(
             y = y_tiles[b, m]
             rows_out = out[b, m * P : (m + 1) * P, :]
             width = NT // pieces
-            last = j == UNITS - 1
+            last = j >= UNITS - 3
             for c in range(pieces):
                 cols = slice(d * NT + c * width, d * NT + (c + 1) * width)
-                nc.vector.tensor_tensor(
-                    out=y[:, cols], in0=banks[j, i][:, c * width : (c + 1) * width], in1=bias_t[:, cols], op=ADD
-                )
+                acc = banks[j, i][:, c * width : (c + 1) * width]
+                if (j, i) in BY_SCALAR:
+                    nc.scalar.copy(out=y[:, cols], in_=acc)
+                    nc.gpsimd.tensor_tensor(out=y[:, cols], in0=y[:, cols], in1=bias_t[:, cols], op=ADD)
+                else:
+                    nc.vector.tensor_tensor(out=y[:, cols], in0=acc, in1=bias_t[:, cols], op=ADD)
                 if last:
-                    engine = nc.scalar if (i + c) % 2 else nc.sync
-                    engine.dma_start(out=rows_out[:, cols], in_=y[:, cols])
+                    if (j, i) in BY_SCALAR:
+                        late.append((rows_out[:, cols], y[:, cols]))
+                    else:
+                        nc.sync.dma_start(out=rows_out[:, cols], in_=y[:, cols])
             if not last and d == D // NT - 1:
                 nc.sync.dma_start(out=rows_out, in_=y[:])
 
@@ -213,14 +239,13 @@ def tile_lag_channel_mixer_s4_kernel(
         regroup_scales(0, 1, 4)
         stage1(0)
         regroup(1)
-        zero(xs_raw[4][:].rearrange("p k n -> p (k n)"))
-        load_x_scales(2)
-        load_x(3)
+        zero(xs_late[:].rearrange("p u k t m -> p (u k t m)"))
         stage1(1)
         regroup_words(2)
         interleave(vcopy, 0, 0, H)
         regroup_scales(2)
         quantise(0, 0)
+        regroup_packed_scales()
         quantise(0, 1)
         stage1(2)
         interleave(vcopy, 1, 0, HALF)
@@ -240,19 +265,27 @@ def tile_lag_channel_mixer_s4_kernel(
                 interleave(vcopy, u - 1, H - V_SHARE, H)
             quantise(u - 1, 0)
             if u + 1 < UNITS:
-                regroup(u + 1)
+                regroup_words(u + 1)
             quantise(u - 1, 1)
             stage2(u - 2)
-            interleave(scopy, u, 0, HALF)
-            interleave(scopy, u, HALF, H - V_SHARE if u < UNITS - 1 else H)
+            if u < UNITS - 1:
+                interleave(scopy, u, 0, HALF)
+                interleave(scopy, u, HALF, H - V_SHARE)
+        for m in range(4):
+            interleave(scopy, 7, m * P, (m + 1) * P)
         finish(5, 0)
         finish(5, 1)
-        quantise(7, 0)
-        stage2(6)
+        quantise(7, 0, P)
         finish(5, 2)
+        quantise(7, 1, P)
         finish(5, 3)
+        stage2(6)
+        finish(6, 0)
         quantise(7, 1)
         stage2(7)
-        for j in (6, 7):
-            for i in range(4):
-                finish(j, i, 2 if (j, i) == (7, 3) else 1)
+        for i in range(1, 4):
+            finish(6, i)
+        for dst, src in late:
+            nc.scalar.dma_start(out=dst, in_=src)
+        for i in range(4):
+            finish(7, i, 2 if i == 3 else 1)

@@ -90,6 +90,36 @@ def tile_lag_channel_mixer_s4_kernel(
         load_x_scales(0)
         for q in range(4):
             load_scales(nc.scalar, lag_s, lag_scales, q)
+
+        def warm_up(passes):
+            zeros = xs_raw[2]
+            for i in range(passes):
+                nc.tensor.matmul_mx(
+                    out=warm_bank[:],
+                    lhsT=zeros[:, 0, 0:256].bitcast(FP4X4),
+                    lhsT_scale=zeros[:, 1, 0:P],
+                    rhs=zeros[:, 0, :].bitcast(FP4X4),
+                    rhs_scale=zeros[:, 1, 0:NT],
+                    start=True,
+                    stop=True,
+                )
+
+        warm_bank = psum.tile([P, NT], F32, name="acc")
+        warm_up(4)
+        bias_bank = psum.tile([P, D // NT, 4, P], BF16, name="acc")
+        for d in range(D // NT):
+            for c in range(4):
+                nc.tensor.transpose(bias_bank[:, d, c, :], bias_cols[:, d, c : c + 1].to_broadcast([P, P]), ident[:])
+        level_bank = psum.tile([P, 4, P], BF16, name="acc")
+        for t in range(4):
+            nc.tensor.transpose(level_bank[:, t, :], level_rows[:, t:512:4], ident[:])
+        warm_up(2)
+        nc.scalar.copy(
+            out=bias_t[:].rearrange("p (d n c) -> p d n c", d=D // NT, c=4),
+            in_=bias_bank[:].rearrange("p d c n -> p d n c"),
+        )
+        nc.scalar.copy(out=lvl[:], in_=level_bank[:, :, 0:UNITS])
+
         load_x(1)
         load_x_scales(1)
         for k in range(KG):
@@ -103,19 +133,6 @@ def tile_lag_channel_mixer_s4_kernel(
         nc.sync.dma_start(out=w_w[:].bitcast(I32), in_=w_words.rearrange("g p n t -> p g (n t)").bitcast(I32))
         load_x(2)
         load_x(3)
-
-        bias_bank = psum.tile([P, D // NT, 4, P], BF16, name="acc")
-        for d in range(D // NT):
-            for c in range(4):
-                nc.tensor.transpose(bias_bank[:, d, c, :], bias_cols[:, d, c : c + 1].to_broadcast([P, P]), ident[:])
-        level_bank = psum.tile([P, 4, P], BF16, name="acc")
-        for t in range(4):
-            nc.tensor.transpose(level_bank[:, t, :], level_rows[:, t:512:4], ident[:])
-        nc.scalar.copy(
-            out=bias_t[:].rearrange("p (d n c) -> p d n c", d=D // NT, c=4),
-            in_=bias_bank[:].rearrange("p d c n -> p d n c"),
-        )
-        nc.scalar.copy(out=lvl[:], in_=level_bank[:, :, 0:UNITS])
 
         def regroup_words(u):
             u0 = max(first for first, n in X_LOADS if first <= u)

@@ -27,7 +27,7 @@ X_LOADS = ((0, 1), (1, 2), (3, 1), (4, 4))
 XS_LOADS = ((0, 2), (2, 2))
 PACKED = 4
 V_SHARE = 192
-BY_SCALAR = ((6, 1), (6, 3))
+BY_SCALAR = ()
 
 
 def tile_lag_channel_mixer_s4_kernel(
@@ -43,7 +43,7 @@ def tile_lag_channel_mixer_s4_kernel(
 
         lag_w = keep.tile([P, KG, 2 * H], U8, align_bytes=64, name="lag_w")
         lag_s = keep.tile([P, KG, H], U8, align_bytes=64, name="lag_s")
-        w_w = keep.tile([P, CG, 4 * D], U8, align_bytes=64, name="w_w")
+        w_w = [keep.tile([P, 4 * D], U8, align_bytes=64, name="w_w%d" % g) for g in range(CG)]
         w_s = keep.tile([P, D], U8, align_bytes=64, name="w_s")
         lvl = keep.tile([P, 4, UNITS], F32, align_bytes=64, name="lvl")
         level_rows = keep.tile([P, 512], BF16, align_bytes=64, name="level_rows")
@@ -51,9 +51,9 @@ def tile_lag_channel_mixer_s4_kernel(
         ident = keep.tile([P, P], BF16, align_bytes=64, name="ident")
         bias_t = keep.tile([P, D], BF16, align_bytes=64, name="bias_t")
         x_raw = {u0: keep.tile([P, KG, n * 1024], U8, align_bytes=64, name="x_raw%d" % u0) for u0, n in X_LOADS}
-        x_st = [keep.tile([P, KG, 4, 256], U8, align_bytes=64, name="x_st%d" % u) for u in range(UNITS)]
+        x_st = [keep.tile([P, 4, KG, 256], U8, align_bytes=64, name="x_st%d" % u) for u in range(UNITS)]
         xs_raw = {u0: keep.tile([P, KG, n * 512], U8, align_bytes=64, name="xs_raw%d" % u0) for u0, n in XS_LOADS}
-        xs_st = [keep.tile([P, KG, 4, P], U8, align_bytes=64, name="xs_st%d" % u) for u in range(PACKED)]
+        xs_st = [keep.tile([P, 4, KG, P], U8, align_bytes=64, name="xs_st%d" % u) for u in range(PACKED)]
         pk_raw = keep.tile([P, 512], U8, align_bytes=64, name="pk_raw")
         pk_st = keep.tile([P, 4, P], U8, align_bytes=64, name="pk_st")
         xs_late = keep.tile([P, UNITS - PACKED, KG, 4, P], U8, align_bytes=64, name="xs_late")
@@ -69,6 +69,9 @@ def tile_lag_channel_mixer_s4_kernel(
             rows = src[:, 4 * q : 4 * q + 4, :].bitcast(I32)
             engine.dma_start(out=dst[32 * q : 32 * q + 4].bitcast(I32), in_=rows.rearrange("k r n -> r k n"))
 
+        def load_w(g):
+            nc.sync.dma_start(out=w_w[g][:].bitcast(I32), in_=w_words[g].rearrange("p n t -> p (n t)").bitcast(I32))
+
         def zero(tile):
             nc.vector.memset(tile.bitcast(I32), 0)
 
@@ -79,27 +82,29 @@ def tile_lag_channel_mixer_s4_kernel(
 
         zero(xs_raw[0][:].rearrange("p k n -> p (k n)"))
         zero(lag_s[:].rearrange("p k n -> p (k n)"))
+        zero(xs_late[:, 0].rearrange("p k t m -> p (k t m)"))
         zero(xs_raw[2][:].rearrange("p k n -> p (k n)"))
         zero(w_s[:])
-        nc.scalar.dma_start(out=bias_cols[:], in_=bias.rearrange("(d p c) -> p d c", p=P, c=4))
+        zero(xs_late[:, 1:4].rearrange("p u k t m -> p (u k t m)"))
+        nc.sync.dma_start(out=bias_cols[:], in_=bias.rearrange("(d p c) -> p d c", p=P, c=4))
         nc.gpsimd.memset(level_rows[:].bitcast(I32), 0)
         nc.gpsimd.dma_start(out=level_rows[0:UNITS, :], in_=level.rearrange("b (g n) -> (b g) n", g=CG))
         make_identity(nc, ident[:])
         load_x(0)
-        nc.scalar.dma_start(out=lag_w[:].bitcast(I32), in_=lag_words[:, :, :].bitcast(I32).rearrange("k p n -> p k n"))
+        nc.sync.dma_start(out=lag_w[:].bitcast(I32), in_=lag_words[:, :, :].bitcast(I32).rearrange("k p n -> p k n"))
         load_x_scales(0)
         for q in range(4):
-            load_scales(nc.scalar, lag_s, lag_scales, q)
+            load_scales(nc.sync, lag_s, lag_scales, q)
 
         def warm_up(passes):
-            zeros = xs_raw[2]
+            zeros = xs_late[:].rearrange("p u k t m -> p (u k t m)")
             for i in range(passes):
                 nc.tensor.matmul_mx(
                     out=warm_bank[:],
-                    lhsT=zeros[:, 0, 0:256].bitcast(FP4X4),
-                    lhsT_scale=zeros[:, 1, 0:P],
-                    rhs=zeros[:, 0, :].bitcast(FP4X4),
-                    rhs_scale=zeros[:, 1, 0:NT],
+                    lhsT=zeros[:, 0:256].bitcast(FP4X4),
+                    lhsT_scale=zeros[:, 0:P],
+                    rhs=zeros[:, 0:1024].bitcast(FP4X4),
+                    rhs_scale=zeros[:, 0:NT],
                     start=True,
                     stop=True,
                 )
@@ -122,15 +127,16 @@ def tile_lag_channel_mixer_s4_kernel(
 
         load_x(1)
         load_x_scales(1)
-        for k in range(KG):
-            rows_k = x_scales[k, :, PACKED * 512 : UNITS * 512].bitcast(I32)
-            nc.sync.dma_start(out=pk_raw[k:P:KG, :].bitcast(I32), in_=rows_k.rearrange("q (u n) -> q u n", n=P))
+        load_w(0)
         for q in range(4):
             nc.sync.dma_start(
                 out=w_s[32 * q : 32 * q + 4 * CG, :].bitcast(I32),
                 in_=w_scales[:, 4 * q : 4 * q + 4, :].bitcast(I32),
             )
-        nc.sync.dma_start(out=w_w[:].bitcast(I32), in_=w_words.rearrange("g p n t -> p g (n t)").bitcast(I32))
+        load_w(1)
+        for k in range(KG):
+            rows_k = x_scales[k, :, PACKED * 512 : UNITS * 512].bitcast(I32)
+            nc.sync.dma_start(out=pk_raw[k:P:KG, :].bitcast(I32), in_=rows_k.rearrange("q (u n) -> q u n", n=P))
         load_x(2)
         load_x(3)
 
@@ -138,13 +144,13 @@ def tile_lag_channel_mixer_s4_kernel(
             u0 = max(first for first, n in X_LOADS if first <= u)
             nc.vector.tensor_copy(
                 out=x_st[u][:].bitcast(U16),
-                in_=x_raw[u0][:, :, (u - u0) * 1024 : (u - u0 + 1) * 1024].bitcast(U16).rearrange("p k (m t) -> p k t m", t=4),
+                in_=x_raw[u0][:, :, (u - u0) * 1024 : (u - u0 + 1) * 1024].bitcast(U16).rearrange("p k (m t) -> p t k m", t=4),
             )
 
         def regroup_scales(u, t0=0, t1=4):
             u0 = max(first for first, n in XS_LOADS if first <= u)
             raw = xs_raw[u0][:, :, (u - u0) * 512 : (u - u0 + 1) * 512]
-            nc.vector.tensor_copy(out=xs_st[u][:, :, t0:t1], in_=raw.rearrange("p k (m t) -> p k t m", t=4)[:, :, t0:t1])
+            nc.vector.tensor_copy(out=xs_st[u][:, t0:t1], in_=raw.rearrange("p k (m t) -> p t k m", t=4)[:, t0:t1])
 
         def regroup(u):
             regroup_words(u)
@@ -159,7 +165,7 @@ def tile_lag_channel_mixer_s4_kernel(
                 )
 
         def x_scale(u, k, t):
-            return xs_st[u][:, k, t, :] if u < PACKED else xs_late[:, u - PACKED, k, t, :]
+            return xs_st[u][:, t, k, :] if u < PACKED else xs_late[:, u - PACKED, k, t, :]
 
         rows = {}
         inter = {}
@@ -171,7 +177,7 @@ def tile_lag_channel_mixer_s4_kernel(
                 for k in range(KG):
                     nc.tensor.matmul_mx(
                         out=acc[:],
-                        lhsT=x_st[u][:, k, t, :].bitcast(FP4X4),
+                        lhsT=x_st[u][:, t, k, :].bitcast(FP4X4),
                         lhsT_scale=x_scale(u, k, t),
                         rhs=lag_w[:, k, :].bitcast(FP4X4),
                         rhs_scale=lag_s[:, k, :],
@@ -209,7 +215,7 @@ def tile_lag_channel_mixer_s4_kernel(
                 out=banks[j, i][:],
                 lhsT=codes[u][:, m * P : (m + 1) * P].bitcast(FP8X4),
                 lhsT_scale=code_scales[u][:, m * P : (m + 1) * P],
-                rhs=w_w[:, g, 4 * d * NT : 4 * (d + 1) * NT].bitcast(FP8X4),
+                rhs=w_w[g][:, 4 * d * NT : 4 * (d + 1) * NT].bitcast(FP8X4),
                 rhs_scale=w_s[4 * g : P, d * NT : (d + 1) * NT],
                 start=(g == 0),
                 stop=(g == CG - 1),
@@ -252,25 +258,23 @@ def tile_lag_channel_mixer_s4_kernel(
         vcopy, scopy = nc.vector.tensor_copy, nc.scalar.copy
 
         regroup_words(0)
-        regroup_scales(0, 0, 1)
-        regroup_scales(0, 1, 4)
+        regroup_scales(0, 0, 2)
+        regroup_scales(0, 2, 4)
         stage1(0)
-        regroup(1)
-        zero(xs_late[:].rearrange("p u k t m -> p (u k t m)"))
+        regroup_scales(1)
+        regroup_words(1)
         stage1(1)
-        regroup_words(2)
-        interleave(vcopy, 0, 0, H)
-        regroup_scales(2)
-        quantise(0, 0)
-        regroup_packed_scales()
-        quantise(0, 1)
+        regroup(2)
+        interleave(vcopy, 0, 0, HALF)
         stage1(2)
+        interleave(vcopy, 0, HALF, H)
+        quantise(0, 0)
         interleave(vcopy, 1, 0, HALF)
-        interleave(vcopy, 1, HALF, H)
+        quantise(0, 1)
+        regroup_packed_scales()
         quantise(1, 0)
-        regroup_scales(3)
-        quantise(1, 1)
-        regroup_words(3)
+        regroup(3)
+        interleave(vcopy, 1, HALF, H)
         stage2(0, group_first=True)
         interleave(scopy, 2, 0, HALF)
         interleave(scopy, 2, HALF, H)
@@ -278,9 +282,11 @@ def tile_lag_channel_mixer_s4_kernel(
             stage1(u)
             for i in range(4):
                 finish(u - 3, i)
+                if (u, i) == (3, 0):
+                    quantise(1, 1)
+            quantise(u - 1, 0)
             if u > 3:
                 interleave(vcopy, u - 1, H - V_SHARE, H)
-            quantise(u - 1, 0)
             if u + 1 < UNITS:
                 regroup_words(u + 1)
             quantise(u - 1, 1)

@@ -18,16 +18,22 @@ ADD = mybir.AluOpType.add
 RELU = mybir.ActivationFunctionType.Relu
 
 P = 128
-KG = L // 512
-CG = C // 512
+SLOTS = 4
+PASS = P * SLOTS
+KG = L // PASS
+CG = C // PASS
 UNITS = B * CG
-NT = 512
+LAST = UNITS - 1
+BANK = 512
+DT = D // BANK
 HALF = H // 2
-X_LOADS = ((0, 1), (1, 2), (3, 1), (4, 4))
+HALF_BANKS = (HALF // P) * DT
+QUADS = 4
+
+X_LOADS = ((0, 1), (1, 1), (2, 2), (4, 4))
 XS_LOADS = ((0, 2), (2, 2))
 PACKED = 4
 V_SHARE = 192
-BY_SCALAR = ()
 
 
 def tile_lag_channel_mixer_s4_kernel(
@@ -41,274 +47,281 @@ def tile_lag_channel_mixer_s4_kernel(
         psum = ctx.enter_context(tc.psum_pool(name="psum", bufs=8))
         ctx.enter_context(tc.manual_schedule())
 
-        lag_w = keep.tile([P, KG, 2 * H], U8, align_bytes=64, name="lag_w")
-        lag_s = keep.tile([P, KG, H], U8, align_bytes=64, name="lag_s")
-        w_w = [keep.tile([P, 4 * D], U8, align_bytes=64, name="w_w%d" % g) for g in range(CG)]
-        w_s = keep.tile([P, D], U8, align_bytes=64, name="w_s")
-        lvl = keep.tile([P, 4, UNITS], F32, align_bytes=64, name="lvl")
-        level_rows = keep.tile([P, 512], BF16, align_bytes=64, name="level_rows")
-        bias_cols = keep.tile([P, D // NT, 4], BF16, align_bytes=64, name="bias_cols")
-        ident = keep.tile([P, P], BF16, align_bytes=64, name="ident")
-        bias_t = keep.tile([P, D], BF16, align_bytes=64, name="bias_t")
-        x_raw = {u0: keep.tile([P, KG, n * 1024], U8, align_bytes=64, name="x_raw%d" % u0) for u0, n in X_LOADS}
-        x_st = [keep.tile([P, 4, KG, 256], U8, align_bytes=64, name="x_st%d" % u) for u in range(UNITS)]
-        xs_raw = {u0: keep.tile([P, KG, n * 512], U8, align_bytes=64, name="xs_raw%d" % u0) for u0, n in XS_LOADS}
-        xs_st = [keep.tile([P, 4, KG, P], U8, align_bytes=64, name="xs_st%d" % u) for u in range(PACKED)]
-        pk_raw = keep.tile([P, 512], U8, align_bytes=64, name="pk_raw")
-        pk_st = keep.tile([P, 4, P], U8, align_bytes=64, name="pk_st")
-        xs_late = keep.tile([P, UNITS - PACKED, KG, 4, P], U8, align_bytes=64, name="xs_late")
-        codes = [keep.tile([P, H], U32, align_bytes=64, name="codes%d" % u) for u in range(UNITS)]
-        code_scales = [keep.tile([P, H], U8, align_bytes=64, name="cs%d" % u) for u in range(UNITS)]
+        def kept(shape, dtype, name):
+            return keep.tile(shape, dtype, align_bytes=64, name=name)
+
+        lag_w = kept([P, KG, 2 * H], U8, "lag_w")
+        lag_s = kept([P, KG, H], U8, "lag_s")
+        w_w = [kept([P, SLOTS * D], U8, "w_w%d" % g) for g in range(CG)]
+        w_s = kept([P, D], U8, "w_s")
+        x_raw = {u0: kept([P, KG, n * 2 * PASS], U8, "x_raw%d" % u0) for u0, n in X_LOADS}
+        x_st = [kept([P, SLOTS, KG, 2 * P], U8, "x_st%d" % u) for u in range(UNITS)]
+        xs_raw = {u0: kept([P, KG, n * PASS], U8, "xs_raw%d" % u0) for u0, n in XS_LOADS}
+        xs_st = [kept([P, SLOTS, KG, P], U8, "xs_st%d" % u) for u in range(PACKED)]
+        packed_raw = kept([P, PASS], U8, "packed_raw")
+        packed_st = kept([P, SLOTS, P], U8, "packed_st")
+        xs_late = kept([P, UNITS - PACKED, KG * PASS], U8, "xs_late")
+        codes = [kept([P, H], U32, "codes%d" % u) for u in range(UNITS)]
+        code_scales = [kept([P, H], U8, "code_scales%d" % u) for u in range(UNITS)]
+        ident = kept([P, P], BF16, "ident")
+        level_rows = kept([P, PASS], BF16, "level_rows")
+        level_cols = kept([P, SLOTS, UNITS], F32, "level_cols")
+        bias_cols = kept([P, DT, SLOTS], BF16, "bias_cols")
+        bias_rows = kept([P, D], BF16, "bias_rows")
 
         def load_x(index):
             u0, n = X_LOADS[index]
-            src = x_words[:, :, u0 * 1024 : (u0 + n) * 1024].bitcast(I32)
+            src = x_words[:, :, u0 * 2 * PASS : (u0 + n) * 2 * PASS].bitcast(I32)
             nc.sync.dma_start(out=x_raw[u0][:].bitcast(I32), in_=src.rearrange("k p n -> p k n"))
 
-        def load_scales(engine, dst, src, q):
-            rows = src[:, 4 * q : 4 * q + 4, :].bitcast(I32)
-            engine.dma_start(out=dst[32 * q : 32 * q + 4].bitcast(I32), in_=rows.rearrange("k r n -> r k n"))
+        def load_scale_rows(dst, src):
+            for q in range(QUADS):
+                rows_q = src[:, 4 * q : 4 * q + 4, :].bitcast(I32)
+                nc.sync.dma_start(out=dst[32 * q : 32 * q + 4].bitcast(I32), in_=rows_q.rearrange("k r n -> r k n"))
+
+        def load_x_scales(index):
+            u0, n = XS_LOADS[index]
+            load_scale_rows(xs_raw[u0], x_scales[:, :, u0 * PASS : (u0 + n) * PASS])
+
+        def load_packed_scales():
+            for k in range(KG):
+                rows_k = x_scales[k, :, PACKED * PASS : UNITS * PASS].bitcast(I32)
+                nc.sync.dma_start(
+                    out=packed_raw[k:P:KG, :].bitcast(I32), in_=rows_k.rearrange("q (u n) -> q u n", u=UNITS - PACKED)
+                )
 
         def load_w(g):
             nc.sync.dma_start(out=w_w[g][:].bitcast(I32), in_=w_words[g].rearrange("p n t -> p (n t)").bitcast(I32))
 
-        def zero(tile):
-            nc.vector.memset(tile.bitcast(I32), 0)
+        def load_w_scales():
+            for q in range(QUADS):
+                nc.sync.dma_start(
+                    out=w_s[32 * q : 32 * q + 4 * CG, :].bitcast(I32),
+                    in_=w_scales[:, 4 * q : 4 * q + 4, :].bitcast(I32),
+                )
 
-        def load_x_scales(index):
-            u0, n = XS_LOADS[index]
-            for q in range(4):
-                load_scales(nc.sync, xs_raw[u0], x_scales[:, :, u0 * 512 : (u0 + n) * 512], q)
+        def zero(engine, tile):
+            engine.memset(tile.bitcast(I32), 0)
 
-        zero(xs_raw[0][:].rearrange("p k n -> p (k n)"))
-        zero(lag_s[:].rearrange("p k n -> p (k n)"))
-        zero(xs_late[:, 0].rearrange("p k t m -> p (k t m)"))
-        zero(xs_raw[2][:].rearrange("p k n -> p (k n)"))
-        zero(w_s[:])
-        zero(xs_late[:, 1:4].rearrange("p u k t m -> p (u k t m)"))
-        nc.sync.dma_start(out=bias_cols[:], in_=bias.rearrange("(d p c) -> p d c", p=P, c=4))
-        nc.gpsimd.memset(level_rows[:].bitcast(I32), 0)
-        nc.gpsimd.dma_start(out=level_rows[0:UNITS, :], in_=level.rearrange("b (g n) -> (b g) n", g=CG))
-        make_identity(nc, ident[:])
-        load_x(0)
-        nc.sync.dma_start(out=lag_w[:].bitcast(I32), in_=lag_words[:, :, :].bitcast(I32).rearrange("k p n -> p k n"))
-        load_x_scales(0)
-        for q in range(4):
-            load_scales(nc.sync, lag_s, lag_scales, q)
-
-        def warm_up(passes):
-            zeros = xs_late[:].rearrange("p u k t m -> p (u k t m)")
+        def warm_up(bank, passes):
+            zeros = xs_late[:, 0, :]
             for i in range(passes):
                 nc.tensor.matmul_mx(
-                    out=warm_bank[:],
-                    lhsT=zeros[:, 0:256].bitcast(FP4X4),
+                    out=bank[:],
+                    lhsT=zeros[:, 0 : 2 * P].bitcast(FP4X4),
                     lhsT_scale=zeros[:, 0:P],
-                    rhs=zeros[:, 0:1024].bitcast(FP4X4),
-                    rhs_scale=zeros[:, 0:NT],
+                    rhs=zeros.bitcast(FP4X4),
+                    rhs_scale=zeros[:, 0:BANK],
                     start=True,
                     stop=True,
                 )
 
-        warm_bank = psum.tile([P, NT], F32, name="acc")
-        warm_up(4)
-        bias_bank = psum.tile([P, D // NT, 4, P], BF16, name="acc")
-        for d in range(D // NT):
-            for c in range(4):
-                nc.tensor.transpose(bias_bank[:, d, c, :], bias_cols[:, d, c : c + 1].to_broadcast([P, P]), ident[:])
-        level_bank = psum.tile([P, 4, P], BF16, name="acc")
-        for t in range(4):
-            nc.tensor.transpose(level_bank[:, t, :], level_rows[:, t:512:4], ident[:])
-        warm_up(2)
-        nc.scalar.copy(
-            out=bias_t[:].rearrange("p (d n c) -> p d n c", d=D // NT, c=4),
-            in_=bias_bank[:].rearrange("p d c n -> p d n c"),
-        )
-        nc.scalar.copy(out=lvl[:], in_=level_bank[:, :, 0:UNITS])
-
-        load_x(1)
-        load_x_scales(1)
-        load_w(0)
-        for q in range(4):
-            nc.sync.dma_start(
-                out=w_s[32 * q : 32 * q + 4 * CG, :].bitcast(I32),
-                in_=w_scales[:, 4 * q : 4 * q + 4, :].bitcast(I32),
+        def spread_bias():
+            bank = psum.tile([P, DT, SLOTS, P], BF16, name="acc")
+            for d in range(DT):
+                for c in range(SLOTS):
+                    nc.tensor.transpose(bank[:, d, c, :], bias_cols[:, d, c : c + 1].to_broadcast([P, P]), ident[:])
+            nc.scalar.copy(
+                out=bias_rows[:].rearrange("p (d n c) -> p d n c", d=DT, c=SLOTS),
+                in_=bank[:].rearrange("p d c n -> p d n c"),
             )
-        load_w(1)
-        for k in range(KG):
-            rows_k = x_scales[k, :, PACKED * 512 : UNITS * 512].bitcast(I32)
-            nc.sync.dma_start(out=pk_raw[k:P:KG, :].bitcast(I32), in_=rows_k.rearrange("q (u n) -> q u n", n=P))
-        load_x(2)
-        load_x(3)
+
+        def turn_level():
+            bank = psum.tile([P, SLOTS, P], BF16, name="acc")
+            for t in range(SLOTS):
+                nc.tensor.transpose(bank[:, t, :], level_rows[:, t:PASS:SLOTS], ident[:])
+            nc.scalar.copy(out=level_cols[:], in_=bank[:, :, 0:UNITS])
 
         def regroup_words(u):
             u0 = max(first for first, n in X_LOADS if first <= u)
+            raw = x_raw[u0][:, :, (u - u0) * 2 * PASS : (u - u0 + 1) * 2 * PASS].bitcast(U16)
+            nc.vector.tensor_copy(out=x_st[u][:].bitcast(U16), in_=raw.rearrange("p k (m t) -> p t k m", t=SLOTS))
+
+        def regroup_scales(u, t0=0, t1=SLOTS):
+            u0 = max(first for first, n in XS_LOADS if first <= u)
+            raw = xs_raw[u0][:, :, (u - u0) * PASS : (u - u0 + 1) * PASS]
             nc.vector.tensor_copy(
-                out=x_st[u][:].bitcast(U16),
-                in_=x_raw[u0][:, :, (u - u0) * 1024 : (u - u0 + 1) * 1024].bitcast(U16).rearrange("p k (m t) -> p t k m", t=4),
+                out=xs_st[u][:, t0:t1], in_=raw.rearrange("p k (m t) -> p t k m", t=SLOTS)[:, t0:t1]
             )
 
-        def regroup_scales(u, t0=0, t1=4):
-            u0 = max(first for first, n in XS_LOADS if first <= u)
-            raw = xs_raw[u0][:, :, (u - u0) * 512 : (u - u0 + 1) * 512]
-            nc.vector.tensor_copy(out=xs_st[u][:, t0:t1], in_=raw.rearrange("p k (m t) -> p t k m", t=4)[:, t0:t1])
-
-        def regroup(u):
-            regroup_words(u)
-            regroup_scales(u)
-
         def regroup_packed_scales():
-            nc.vector.tensor_copy(out=pk_st[:], in_=pk_raw[:].rearrange("p (m t) -> p t m", t=4))
-            for q in range(4):
+            nc.vector.tensor_copy(out=packed_st[:], in_=packed_raw[:].rearrange("p (m t) -> p t m", t=SLOTS))
+            for q in range(QUADS):
                 nc.sync.dma_start(
-                    out=xs_late[32 * q : 32 * q + 4].rearrange("p u k t m -> p (u k) (t m)").bitcast(I32),
-                    in_=pk_st[32 * q : 32 * q + 32].rearrange("p t m -> p (t m)").bitcast(I32),
+                    out=xs_late[32 * q : 32 * q + 4].rearrange("p u (k n) -> p (u k) n", k=KG).bitcast(I32),
+                    in_=packed_st[32 * q : 32 * q + 32].rearrange("p t m -> p (t m)").bitcast(I32),
                 )
 
         def x_scale(u, k, t):
-            return xs_st[u][:, t, k, :] if u < PACKED else xs_late[:, u - PACKED, k, t, :]
+            if u < PACKED:
+                return xs_st[u][:, t, k, :]
+            return xs_late[:, u - PACKED, k * PASS + t * P : k * PASS + (t + 1) * P]
 
         rows = {}
-        inter = {}
+        words = {}
 
-        def stage1(u):
-            rows[u] = work.tile([P, 4, H], BF16, align_bytes=64, name="rows")
-            for t in range(4):
-                acc = psum.tile([P, NT], F32, name="acc")
+        def stage1(u, h0=0, h1=H):
+            if u not in rows:
+                rows[u] = work.tile([P, SLOTS, H], BF16, align_bytes=64, name="rows")
+            for t in range(SLOTS):
+                acc = psum.tile([P, h1 - h0], F32, name="acc")
                 for k in range(KG):
                     nc.tensor.matmul_mx(
                         out=acc[:],
                         lhsT=x_st[u][:, t, k, :].bitcast(FP4X4),
                         lhsT_scale=x_scale(u, k, t),
-                        rhs=lag_w[:, k, :].bitcast(FP4X4),
-                        rhs_scale=lag_s[:, k, :],
+                        rhs=lag_w[:, k, 2 * h0 : 2 * h1].bitcast(FP4X4),
+                        rhs_scale=lag_s[:, k, h0:h1],
                         start=(k == 0),
                         stop=(k == KG - 1),
                     )
-                nc.scalar.activation(out=rows[u][:, t, :], in_=acc[:], func=RELU, bias=lvl[:, t, u : u + 1])
+                nc.scalar.activation(out=rows[u][:, t, h0:h1], in_=acc[:], func=RELU, bias=level_cols[:, t, u : u + 1])
 
-        def interleave(copy, u, n0, n1):
-            if u not in inter:
-                inter[u] = work.tile([P, H, 4], BF16, align_bytes=64, name="inter")
+        def interleave(copy, u, h0, h1):
+            if u not in words:
+                words[u] = work.tile([P, H, SLOTS], BF16, align_bytes=64, name="words")
             copy(
-                out=inter[u][:, n0:n1, :].rearrange("p (c i) t -> p c t i", i=4),
-                in_=rows[u][:, :, n0:n1].rearrange("p t (c i) -> p c t i", i=4),
+                out=words[u][:, h0:h1, :].rearrange("p (c i) t -> p c t i", i=4),
+                in_=rows[u][:, :, h0:h1].rearrange("p t (c i) -> p c t i", i=4),
             )
 
-        def quantise(u, part, width=HALF):
-            cols = slice(part * width, (part + 1) * width)
+        def quantise(u, h0, h1):
             nc.vector.quantize_mx(
-                out=codes[u][:, cols].bitcast(FP8X4),
-                scales=code_scales[u][:, cols],
-                in_=inter[u][:, cols, :].rearrange("p n t -> p (n t)"),
+                out=codes[u][:, h0:h1].bitcast(FP8X4),
+                scales=code_scales[u][:, h0:h1],
+                in_=words[u][:, h0:h1, :].rearrange("p h t -> p (h t)"),
             )
 
         banks = {}
         y_tiles = {}
-        late = []
+
+        def place(j, i):
+            return j // 2, (HALF // P) * (j % 2) + i // DT, i % DT
 
         def multiply(j, i, g):
-            u = (j // 2) * CG + g
-            m, d = 2 * (j % 2) + i // 2, i % 2
+            b, m, d = place(j, i)
+            u = b * CG + g
             if g == 0:
-                banks[j, i] = psum.tile([P, NT], F32, name="acc")
+                banks[j, i] = psum.tile([P, BANK], F32, name="acc")
             nc.tensor.matmul_mx(
                 out=banks[j, i][:],
                 lhsT=codes[u][:, m * P : (m + 1) * P].bitcast(FP8X4),
                 lhsT_scale=code_scales[u][:, m * P : (m + 1) * P],
-                rhs=w_w[g][:, 4 * d * NT : 4 * (d + 1) * NT].bitcast(FP8X4),
-                rhs_scale=w_s[4 * g : P, d * NT : (d + 1) * NT],
+                rhs=w_w[g][:, SLOTS * d * BANK : SLOTS * (d + 1) * BANK].bitcast(FP8X4),
+                rhs_scale=w_s[4 * g : P, d * BANK : (d + 1) * BANK],
                 start=(g == 0),
                 stop=(g == CG - 1),
             )
 
-        def stage2(j, group_first=False):
-            if group_first:
+        def stage2(j):
+            for i in range(HALF_BANKS):
                 for g in range(CG):
-                    for i in range(4):
-                        multiply(j, i, g)
-            else:
-                for i in range(4):
-                    for g in range(CG):
-                        multiply(j, i, g)
+                    multiply(j, i, g)
 
         def finish(j, i, pieces=1):
-            b, m, d = j // 2, 2 * (j % 2) + i // 2, i % 2
+            b, m, d = place(j, i)
             if d == 0:
                 y_tiles[b, m] = outs.tile([P, D], F32, name="y")
             y = y_tiles[b, m]
             rows_out = out[b, m * P : (m + 1) * P, :]
-            width = NT // pieces
-            last = j >= UNITS - 3
+            width = BANK // pieces
             for c in range(pieces):
-                cols = slice(d * NT + c * width, d * NT + (c + 1) * width)
+                cols = slice(d * BANK + c * width, d * BANK + (c + 1) * width)
                 acc = banks[j, i][:, c * width : (c + 1) * width]
-                if (j, i) in BY_SCALAR:
-                    nc.scalar.copy(out=y[:, cols], in_=acc)
-                    nc.gpsimd.tensor_tensor(out=y[:, cols], in0=y[:, cols], in1=bias_t[:, cols], op=ADD)
-                else:
-                    nc.vector.tensor_tensor(out=y[:, cols], in0=acc, in1=bias_t[:, cols], op=ADD)
-                if last:
-                    if (j, i) in BY_SCALAR:
-                        late.append((rows_out[:, cols], y[:, cols]))
-                    else:
-                        nc.sync.dma_start(out=rows_out[:, cols], in_=y[:, cols])
-            if not last and d == D // NT - 1:
+                nc.vector.tensor_tensor(out=y[:, cols], in0=acc, in1=bias_rows[:, cols], op=ADD)
+                if b == B - 1:
+                    nc.sync.dma_start(out=rows_out[:, cols], in_=y[:, cols])
+            if b < B - 1 and d == DT - 1:
                 nc.sync.dma_start(out=rows_out, in_=y[:])
 
-        vcopy, scopy = nc.vector.tensor_copy, nc.scalar.copy
+        on_vector, on_scalar = nc.vector.tensor_copy, nc.scalar.copy
+
+        zero(nc.vector, xs_raw[0][:].rearrange("p k n -> p (k n)"))
+        zero(nc.vector, lag_s[:].rearrange("p k n -> p (k n)"))
+        zero(nc.vector, level_rows[:])
+        zero(nc.gpsimd, xs_late[:, 0, :])
+        make_identity(nc, ident[:])
+        nc.gpsimd.dma_start(out=level_rows[0:UNITS, :], in_=level.rearrange("b (g n) -> (b g) n", g=CG))
+        nc.sync.dma_start(out=bias_cols[:], in_=bias.rearrange("(d p c) -> p d c", p=P, c=SLOTS))
+        load_x(0)
+        nc.sync.dma_start(out=lag_w[:].bitcast(I32), in_=lag_words[:, :, :].bitcast(I32).rearrange("k p n -> p k n"))
+        load_x_scales(0)
+        load_scale_rows(lag_s, lag_scales)
+        load_x(1)
+        load_x(2)
+        warm_bank = psum.tile([P, BANK], F32, name="acc")
+        warm_up(warm_bank, 4)
+        spread_bias()
+        warm_up(warm_bank, 2)
+        turn_level()
 
         regroup_words(0)
+        zero(nc.vector, xs_raw[2][:].rearrange("p k n -> p (k n)"))
+        zero(nc.vector, w_s[:])
+        load_x_scales(1)
+        load_w(0)
+        load_w_scales()
+        load_w(1)
+        load_packed_scales()
+        load_x(3)
         regroup_scales(0, 0, 2)
-        regroup_scales(0, 2, 4)
+        regroup_scales(0, 2, SLOTS)
         stage1(0)
         regroup_scales(1)
+        zero(nc.vector, xs_late[:, 1:, :].rearrange("p u n -> p (u n)"))
         regroup_words(1)
         stage1(1)
-        regroup(2)
-        interleave(vcopy, 0, 0, HALF)
+        regroup_words(2)
+        regroup_scales(2)
         stage1(2)
-        interleave(vcopy, 0, HALF, H)
-        quantise(0, 0)
-        interleave(vcopy, 1, 0, HALF)
-        quantise(0, 1)
+
+        interleave(on_vector, 0, 0, HALF)
+        interleave(on_vector, 0, HALF, H)
+        quantise(0, 0, HALF)
+        interleave(on_vector, 1, 0, HALF)
+        quantise(0, HALF, H)
         regroup_packed_scales()
-        quantise(1, 0)
-        regroup(3)
-        interleave(vcopy, 1, HALF, H)
-        stage2(0, group_first=True)
-        interleave(scopy, 2, 0, HALF)
-        interleave(scopy, 2, HALF, H)
+        quantise(1, 0, HALF)
+        regroup_words(3)
+        regroup_scales(3)
+        interleave(on_vector, 1, HALF, H)
+        for g in range(CG):
+            for i in range(HALF_BANKS):
+                multiply(0, i, g)
+        interleave(on_scalar, 2, 0, HALF)
+        interleave(on_scalar, 2, HALF, H)
+
         for u in range(3, UNITS):
-            stage1(u)
-            for i in range(4):
+            stage1(u, 0, H if u < LAST else HALF)
+            for i in range(HALF_BANKS):
                 finish(u - 3, i)
-                if (u, i) == (3, 0):
-                    quantise(1, 1)
-            quantise(u - 1, 0)
+                if u == 3 and i == 0:
+                    quantise(1, HALF, H)
+            quantise(u - 1, 0, HALF)
             if u > 3:
-                interleave(vcopy, u - 1, H - V_SHARE, H)
-            if u + 1 < UNITS:
+                interleave(on_vector, u - 1, H - V_SHARE, H)
+            if u < LAST:
                 regroup_words(u + 1)
-            quantise(u - 1, 1)
+            quantise(u - 1, HALF, H)
             stage2(u - 2)
-            if u < UNITS - 1:
-                interleave(scopy, u, 0, HALF)
-                interleave(scopy, u, HALF, H - V_SHARE)
-        for m in range(4):
-            interleave(scopy, 7, m * P, (m + 1) * P)
-        finish(5, 0)
-        finish(5, 1)
-        quantise(7, 0, P)
-        finish(5, 2)
-        quantise(7, 1, P)
-        finish(5, 3)
-        stage2(6)
-        finish(6, 0)
-        quantise(7, 1)
-        stage2(7)
-        for i in range(1, 4):
-            finish(6, i)
-        for dst, src in late:
-            nc.scalar.dma_start(out=dst, in_=src)
-        for i in range(4):
-            finish(7, i, 2 if i == 3 else 1)
+            interleave(on_scalar, u, 0, HALF)
+            if u < LAST:
+                interleave(on_scalar, u, HALF, H - V_SHARE)
+
+        stage1(LAST, HALF, H)
+        for i in range(HALF_BANKS - 1):
+            finish(LAST - 2, i)
+        quantise(LAST, 0, HALF)
+        finish(LAST - 2, HALF_BANKS - 1)
+        stage2(LAST - 1)
+        interleave(on_scalar, LAST, HALF, HALF + P)
+        interleave(on_scalar, LAST, HALF + P, H)
+        finish(LAST - 1, 0)
+        finish(LAST - 1, 1)
+        quantise(LAST, HALF, HALF + P)
+        finish(LAST - 1, 2)
+        quantise(LAST, HALF + P, H)
+        finish(LAST - 1, 3)
+        stage2(LAST)
+        for i in range(HALF_BANKS):
+            finish(LAST, i, 2 if i == HALF_BANKS - 1 else 1)

@@ -33,7 +33,7 @@ QUADS = 4
 X_LOADS = ((0, 1), (1, 1), (2, 2), (4, 4))
 XS_LOADS = ((0, 2), (2, 2))
 PACKED = 4
-V_SHARE = 192
+V_SHARE = 224
 
 
 def tile_lag_channel_mixer_s4_kernel(
@@ -276,15 +276,15 @@ def tile_lag_channel_mixer_s4_kernel(
         stage1(2)
 
         interleave(on_vector, 0, 0, HALF)
-        interleave(on_vector, 0, HALF, H)
+        regroup_words(3)
         quantise(0, 0, HALF)
+        regroup_scales(3)
         interleave(on_vector, 1, 0, HALF)
-        quantise(0, HALF, H)
         regroup_packed_scales()
         quantise(1, 0, HALF)
-        regroup_words(3)
-        regroup_scales(3)
+        interleave(on_vector, 0, HALF, H)
         interleave(on_vector, 1, HALF, H)
+        quantise(0, HALF, H)
         for g in range(CG):
             for i in range(HALF_BANKS):
                 multiply(0, i, g)
@@ -298,21 +298,21 @@ def tile_lag_channel_mixer_s4_kernel(
                 if u == 3 and i == 0:
                     quantise(1, HALF, H)
             quantise(u - 1, 0, HALF)
-            if u > 3:
-                interleave(on_vector, u - 1, H - V_SHARE, H)
             if u < LAST:
+                if u > 3:
+                    interleave(on_vector, u - 1, H - V_SHARE, H)
                 regroup_words(u + 1)
-            quantise(u - 1, HALF, H)
+                quantise(u - 1, HALF, H)
             stage2(u - 2)
-            interleave(on_scalar, u, 0, HALF)
-            if u < LAST:
-                interleave(on_scalar, u, HALF, H - V_SHARE)
+            interleave(on_scalar, u, 0, H - V_SHARE if u < LAST - 1 else HALF)
 
         stage1(LAST, HALF, H)
+        interleave(on_vector, LAST - 1, HALF, H)
         for i in range(HALF_BANKS - 1):
             finish(LAST - 2, i)
         quantise(LAST, 0, HALF)
         finish(LAST - 2, HALF_BANKS - 1)
+        quantise(LAST - 1, HALF, H)
         stage2(LAST - 1)
         interleave(on_scalar, LAST, HALF, HALF + P)
         interleave(on_scalar, LAST, HALF + P, H)
@@ -322,6 +322,11 @@ def tile_lag_channel_mixer_s4_kernel(
         finish(LAST - 1, 2)
         quantise(LAST, HALF + P, H)
         finish(LAST - 1, 3)
-        stage2(LAST)
+        for g in range(CG):
+            for i in range(DT):
+                multiply(LAST, i, g)
+        for i in range(DT, HALF_BANKS):
+            for g in range(CG):
+                multiply(LAST, i, g)
         for i in range(HALF_BANKS):
             finish(LAST, i, 2 if i == HALF_BANKS - 1 else 1)

@@ -30,7 +30,7 @@ HALF = H // 2
 HALF_BANKS = (HALF // P) * DT
 QUADS = 4
 
-X_LOADS = ((0, 1), (1, 1), (2, 2), (4, 4))
+X_LOADS = ((0, 1), (1, 1), (2, 2), (4, 2), (6, 2))
 XS_LOADS = ((0, 2), (2, 2))
 PACKED = 4
 V_SHARE = 224
@@ -75,9 +75,9 @@ def tile_lag_channel_mixer_s4_kernel(
             nc.sync.dma_start(out=x_raw[u0][:].bitcast(I32), in_=src.rearrange("k p n -> p k n"))
 
         def load_scale_rows(dst, src):
-            for q in range(QUADS):
-                rows_q = src[:, 4 * q : 4 * q + 4, :].bitcast(I32)
-                nc.sync.dma_start(out=dst[32 * q : 32 * q + 4].bitcast(I32), in_=rows_q.rearrange("k r n -> r k n"))
+            for r in range(4):
+                rows_r = src[:, r:16:4, :].bitcast(I32)
+                nc.sync.dma_start(out=dst[r:P:32].bitcast(I32), in_=rows_r.rearrange("k q n -> q k n"))
 
         def load_x_scales(index):
             u0, n = XS_LOADS[index]
@@ -146,7 +146,7 @@ def tile_lag_channel_mixer_s4_kernel(
 
         def regroup_packed_scales():
             nc.vector.tensor_copy(out=packed_st[:], in_=packed_raw[:].rearrange("p (m t) -> p t m", t=SLOTS))
-            for q in range(QUADS):
+            for q in (0, 2, 1, 3):
                 nc.sync.dma_start(
                     out=xs_late[32 * q : 32 * q + 4].rearrange("p u (k n) -> p (u k) n", k=KG).bitcast(I32),
                     in_=packed_st[32 * q : 32 * q + 32].rearrange("p t m -> p (t m)").bitcast(I32),
@@ -280,8 +280,9 @@ def tile_lag_channel_mixer_s4_kernel(
         quantise(0, 0, HALF)
         regroup_scales(3)
         interleave(on_vector, 1, 0, HALF)
-        regroup_packed_scales()
         quantise(1, 0, HALF)
+        regroup_packed_scales()
+        load_x(4)
         interleave(on_vector, 0, HALF, H)
         interleave(on_vector, 1, HALF, H)
         quantise(0, HALF, H)

@@ -33,7 +33,7 @@ QUADS = 4
 X_LOADS = ((0, 1), (1, 1), (2, 2), (4, 2), (6, 2))
 XS_LOADS = ((0, 2), (2, 2))
 PACKED = 4
-V_SHARE = 224
+V_SHARE = 128
 
 
 def tile_lag_channel_mixer_s4_kernel(
@@ -60,7 +60,7 @@ def tile_lag_channel_mixer_s4_kernel(
         xs_st = [kept([P, SLOTS, KG, P], U8, "xs_st%d" % u) for u in range(PACKED)]
         packed_raw = kept([P, PASS], U8, "packed_raw")
         packed_st = kept([P, SLOTS, P], U8, "packed_st")
-        xs_late = kept([P, UNITS - PACKED, KG * PASS], U8, "xs_late")
+        xs_late = x_raw[2][:].rearrange("p k (a n) -> p (k a) n", n=KG * PASS)
         codes = [kept([P, H], U32, "codes%d" % u) for u in range(UNITS)]
         code_scales = [kept([P, H], U8, "code_scales%d" % u) for u in range(UNITS)]
         ident = kept([P, P], BF16, "ident")
@@ -104,7 +104,7 @@ def tile_lag_channel_mixer_s4_kernel(
             engine.memset(tile.bitcast(I32), 0)
 
         def warm_up(bank, passes):
-            zeros = xs_late[:, 0, :]
+            zeros = codes[LAST][:, 0 : BANK // 2].bitcast(U8)
             for i in range(passes):
                 nc.tensor.matmul_mx(
                     out=bank[:],
@@ -135,7 +135,10 @@ def tile_lag_channel_mixer_s4_kernel(
         def regroup_words(u):
             u0 = max(first for first, n in X_LOADS if first <= u)
             raw = x_raw[u0][:, :, (u - u0) * 2 * PASS : (u - u0 + 1) * 2 * PASS].bitcast(U16)
-            nc.vector.tensor_copy(out=x_st[u][:].bitcast(U16), in_=raw.rearrange("p k (m t) -> p t k m", t=SLOTS))
+            nc.vector.tensor_copy(
+                out=x_st[u][:].bitcast(U16).rearrange("p t k (c i) -> p k c t i", i=8),
+                in_=raw.rearrange("p k (c i t) -> p k c t i", i=8, t=SLOTS),
+            )
 
         def regroup_scales(u, t0=0, t1=SLOTS):
             u0 = max(first for first, n in XS_LOADS if first <= u)
@@ -239,7 +242,7 @@ def tile_lag_channel_mixer_s4_kernel(
         zero(nc.vector, xs_raw[0][:].rearrange("p k n -> p (k n)"))
         zero(nc.vector, lag_s[:].rearrange("p k n -> p (k n)"))
         zero(nc.vector, level_rows[:])
-        zero(nc.gpsimd, xs_late[:, 0, :])
+        zero(nc.gpsimd, codes[LAST][:, 0 : BANK // 2])
         make_identity(nc, ident[:])
         nc.gpsimd.dma_start(out=level_rows[0:UNITS, :], in_=level.rearrange("b (g n) -> (b g) n", g=CG))
         nc.sync.dma_start(out=bias_cols[:], in_=bias.rearrange("(d p c) -> p d c", p=P, c=SLOTS))
@@ -268,7 +271,6 @@ def tile_lag_channel_mixer_s4_kernel(
         regroup_scales(0, 2, SLOTS)
         stage1(0)
         regroup_scales(1)
-        zero(nc.vector, xs_late[:, 1:, :].rearrange("p u n -> p (u n)"))
         regroup_words(1)
         stage1(1)
         regroup_words(2)
@@ -306,9 +308,11 @@ def tile_lag_channel_mixer_s4_kernel(
                 quantise(u - 1, HALF, H)
             stage2(u - 2)
             interleave(on_scalar, u, 0, H - V_SHARE if u < LAST - 1 else HALF)
+            if u >= LAST - 1:
+                h0 = HALF + (u - LAST + 1) * P
+                interleave(on_scalar, LAST - 1, h0, h0 + P)
 
         stage1(LAST, HALF, H)
-        interleave(on_vector, LAST - 1, HALF, H)
         for i in range(HALF_BANKS - 1):
             finish(LAST - 2, i)
         quantise(LAST, 0, HALF)

@@ -34,6 +34,7 @@ X_LOADS = ((0, 1), (1, 1), (2, 2), (4, 2), (6, 2))
 XS_LOADS = ((0, 2), (2, 2))
 PACKED = 4
 V_SHARE = 128
+BIAS_WORDS = D // P // 2
 
 
 def tile_lag_channel_mixer_s4_kernel(
@@ -63,10 +64,10 @@ def tile_lag_channel_mixer_s4_kernel(
         xs_late = x_raw[2][:].rearrange("p k (a n) -> p (k a) n", n=KG * PASS)
         codes = [kept([P, H], U32, "codes%d" % u) for u in range(UNITS)]
         code_scales = [kept([P, H], U8, "code_scales%d" % u) for u in range(UNITS)]
-        ident = kept([P, P], BF16, "ident")
+        ident = kept([P, P], F32, "ident")
         level_rows = kept([P, PASS], BF16, "level_rows")
-        level_cols = kept([P, SLOTS, UNITS], F32, "level_cols")
-        bias_cols = kept([P, DT, SLOTS], BF16, "bias_cols")
+        level_cols = kept([P, 2, UNITS, 2], F32, "level_cols")
+        bias_cols = kept([P, D // P], BF16, "bias_cols")
         bias_rows = kept([P, D], BF16, "bias_rows")
 
         def load_x(index):
@@ -74,8 +75,8 @@ def tile_lag_channel_mixer_s4_kernel(
             src = x_words[:, :, u0 * 2 * PASS : (u0 + n) * 2 * PASS].bitcast(I32)
             nc.sync.dma_start(out=x_raw[u0][:].bitcast(I32), in_=src.rearrange("k p n -> p k n"))
 
-        def load_scale_rows(dst, src):
-            for r in range(4):
+        def load_scale_rows(dst, src, r0=0, r1=4):
+            for r in range(r0, r1):
                 rows_r = src[:, r:16:4, :].bitcast(I32)
                 nc.sync.dma_start(out=dst[r:P:32].bitcast(I32), in_=rows_r.rearrange("k q n -> q k n"))
 
@@ -117,20 +118,23 @@ def tile_lag_channel_mixer_s4_kernel(
                 )
 
         def spread_bias():
-            bank = psum.tile([P, DT, SLOTS, P], BF16, name="acc")
-            for d in range(DT):
-                for c in range(SLOTS):
-                    nc.tensor.transpose(bank[:, d, c, :], bias_cols[:, d, c : c + 1].to_broadcast([P, P]), ident[:])
+            pairs = bias_cols[:].bitcast(F32)
+            bank = psum.tile([P, BIAS_WORDS, P], F32, name="acc")
+            for c in range(BIAS_WORDS):
+                nc.tensor.transpose(bank[:, c, :], pairs[:, c : c + 1].to_broadcast([P, P]), ident[:])
             nc.scalar.copy(
-                out=bias_rows[:].rearrange("p (d n c) -> p d n c", d=DT, c=SLOTS),
-                in_=bank[:].rearrange("p d c n -> p d n c"),
+                out=bias_rows[:].bitcast(F32).rearrange("p (n c) -> p n c", c=BIAS_WORDS),
+                in_=bank[:].rearrange("p c n -> p n c"),
             )
 
         def turn_level():
-            bank = psum.tile([P, SLOTS, P], BF16, name="acc")
-            for t in range(SLOTS):
-                nc.tensor.transpose(bank[:, t, :], level_rows[:, t:PASS:SLOTS], ident[:])
-            nc.scalar.copy(out=level_cols[:], in_=bank[:, :, 0:UNITS])
+            pairs = level_rows[:].bitcast(F32)
+            bank = psum.tile([P, 2, P], F32, name="acc")
+            for e in range(2):
+                nc.tensor.transpose(bank[:, e, :], pairs[:, e : PASS // 2 : 2], ident[:])
+            nc.scalar.copy(
+                out=level_cols[:].rearrange("p e u i -> p e (u i)"), in_=bank[:].bitcast(BF16)[:, :, 0 : 2 * UNITS]
+            )
 
         def regroup_words(u):
             u0 = max(first for first, n in X_LOADS if first <= u)
@@ -178,7 +182,7 @@ def tile_lag_channel_mixer_s4_kernel(
                         start=(k == 0),
                         stop=(k == KG - 1),
                     )
-                nc.scalar.activation(out=rows[u][:, t, h0:h1], in_=acc[:], func=RELU, bias=level_cols[:, t, u : u + 1])
+                nc.scalar.activation(out=rows[u][:, t, h0:h1], in_=acc[:], func=RELU, bias=level_cols[:, t // 2, u, t % 2 : t % 2 + 1])
 
         def interleave(copy, u, h0, h1):
             if u not in words:
@@ -239,24 +243,24 @@ def tile_lag_channel_mixer_s4_kernel(
 
         on_vector, on_scalar = nc.vector.tensor_copy, nc.scalar.copy
 
-        zero(nc.vector, xs_raw[0][:].rearrange("p k n -> p (k n)"))
-        zero(nc.vector, lag_s[:].rearrange("p k n -> p (k n)"))
         zero(nc.vector, level_rows[:])
-        zero(nc.gpsimd, codes[LAST][:, 0 : BANK // 2])
+        zero(nc.vector, codes[LAST][:, 0 : BANK // 2])
+        zero(nc.vector, lag_s[:].rearrange("p k n -> p (k n)"))
+        zero(nc.vector, xs_raw[0][:].rearrange("p k n -> p (k n)"))
+        nc.gpsimd.dma_start(out=bias_cols[:], in_=bias.rearrange("(p c) -> p c", p=P))
         make_identity(nc, ident[:])
-        nc.gpsimd.dma_start(out=level_rows[0:UNITS, :], in_=level.rearrange("b (g n) -> (b g) n", g=CG))
-        nc.sync.dma_start(out=bias_cols[:], in_=bias.rearrange("(d p c) -> p d c", p=P, c=SLOTS))
         load_x(0)
+        nc.sync.dma_start(out=level_rows[0:UNITS, :], in_=level.rearrange("b (g n) -> (b g) n", g=CG))
+        load_scale_rows(lag_s, lag_scales, 0, 1)
         nc.sync.dma_start(out=lag_w[:].bitcast(I32), in_=lag_words[:, :, :].bitcast(I32).rearrange("k p n -> p k n"))
         load_x_scales(0)
-        load_scale_rows(lag_s, lag_scales)
+        load_scale_rows(lag_s, lag_scales, 1, 4)
         load_x(1)
         load_x(2)
         warm_bank = psum.tile([P, BANK], F32, name="acc")
-        warm_up(warm_bank, 4)
-        spread_bias()
-        warm_up(warm_bank, 2)
+        warm_up(warm_bank, 5)
         turn_level()
+        spread_bias()
 
         regroup_words(0)
         zero(nc.vector, xs_raw[2][:].rearrange("p k n -> p (k n)"))

@@ -1,7 +1,6 @@
 from contextlib import ExitStack
 
 import concourse.mybir as mybir
-from concourse.masks import make_identity
 
 L, H, B, C, D = 1024, 512, 4, 1024, 1024
 FLOPS = 2 * L * H * B * C + 2 * B * H * C * D
@@ -30,11 +29,12 @@ HALF = H // 2
 HALF_BANKS = (HALF // P) * DT
 QUADS = 4
 
-X_LOADS = ((0, 1), (1, 1), (2, 2), (4, 2), (6, 2))
+X_LOADS = ((0, 1), (1, 1), (2, 1), (3, 1), (4, 2), (6, 2))
 XS_LOADS = ((0, 2), (2, 2))
 PACKED = 4
 V_SHARE = 128
-BIAS_WORDS = D // P // 2
+LEVEL_PAD = 16
+SPREAD = 8
 
 
 def tile_lag_channel_mixer_s4_kernel(
@@ -55,25 +55,28 @@ def tile_lag_channel_mixer_s4_kernel(
         lag_s = kept([P, KG, H], U8, "lag_s")
         w_w = [kept([P, SLOTS * D], U8, "w_w%d" % g) for g in range(CG)]
         w_s = kept([P, D], U8, "w_s")
-        x_raw = {u0: kept([P, KG, n * 2 * PASS], U8, "x_raw%d" % u0) for u0, n in X_LOADS}
+        x_raw = {u0: kept([P, KG, n * 2 * PASS], U8, "x_raw%d" % u0)[:] for u0, n in X_LOADS if u0 not in (2, 3)}
+        x_pair = kept([P, 2 * KG * 2 * PASS], U8, "x_pair")
+        for u in (2, 3):
+            x_raw[u] = x_pair[:, (u - 2) * KG * 2 * PASS : (u - 1) * KG * 2 * PASS].rearrange("p (k n) -> p k n", k=KG)
         x_st = [kept([P, SLOTS, KG, 2 * P], U8, "x_st%d" % u) for u in range(UNITS)]
         xs_raw = {u0: kept([P, KG, n * PASS], U8, "xs_raw%d" % u0) for u0, n in XS_LOADS}
         xs_st = [kept([P, SLOTS, KG, P], U8, "xs_st%d" % u) for u in range(PACKED)]
         packed_raw = kept([P, PASS], U8, "packed_raw")
         packed_st = kept([P, SLOTS, P], U8, "packed_st")
-        xs_late = x_raw[2][:].rearrange("p k (a n) -> p (k a) n", n=KG * PASS)
+        xs_late = x_pair[:].rearrange("p (u n) -> p u n", n=KG * PASS)
         codes = [kept([P, H], U32, "codes%d" % u) for u in range(UNITS)]
         code_scales = [kept([P, H], U8, "code_scales%d" % u) for u in range(UNITS)]
-        ident = kept([P, P], F32, "ident")
-        level_rows = kept([P, PASS], BF16, "level_rows")
-        level_cols = kept([P, 2, UNITS, 2], F32, "level_cols")
-        bias_cols = kept([P, D // P], BF16, "bias_cols")
+        level_first = kept([P, CG, LEVEL_PAD], BF16, "level_first")
+        level_rest = kept([P, UNITS - CG, LEVEL_PAD], BF16, "level_rest")
+        level_cols = kept([P, CG, SLOTS], F32, "level_cols")
+        bias_few = kept([P, D], BF16, "bias_few")
         bias_rows = kept([P, D], BF16, "bias_rows")
 
         def load_x(index):
             u0, n = X_LOADS[index]
             src = x_words[:, :, u0 * 2 * PASS : (u0 + n) * 2 * PASS].bitcast(I32)
-            nc.sync.dma_start(out=x_raw[u0][:].bitcast(I32), in_=src.rearrange("k p n -> p k n"))
+            nc.sync.dma_start(out=x_raw[u0].bitcast(I32), in_=src.rearrange("k p n -> p k n"))
 
         def load_scale_rows(dst, src, r0=0, r1=4):
             for r in range(r0, r1):
@@ -117,24 +120,17 @@ def tile_lag_channel_mixer_s4_kernel(
                     stop=True,
                 )
 
-        def spread_bias():
-            pairs = bias_cols[:].bitcast(F32)
-            bank = psum.tile([P, BIAS_WORDS, P], F32, name="acc")
-            for c in range(BIAS_WORDS):
-                nc.tensor.transpose(bank[:, c, :], pairs[:, c : c + 1].to_broadcast([P, P]), ident[:])
-            nc.scalar.copy(
-                out=bias_rows[:].bitcast(F32).rearrange("p (n c) -> p n c", c=BIAS_WORDS),
-                in_=bank[:].rearrange("p c n -> p n c"),
-            )
+        def load_level(dst, src):
+            nc.gpsimd.dma_start(out=dst[:, :, 0:SLOTS], in_=src.rearrange("b (g p t) -> p (b g) t", g=CG, t=SLOTS))
 
-        def turn_level():
-            pairs = level_rows[:].bitcast(F32)
-            bank = psum.tile([P, 2, P], F32, name="acc")
-            for e in range(2):
-                nc.tensor.transpose(bank[:, e, :], pairs[:, e : PASS // 2 : 2], ident[:])
-            nc.scalar.copy(
-                out=level_cols[:].rearrange("p e u i -> p e (u i)"), in_=bank[:].bitcast(BF16)[:, :, 0 : 2 * UNITS]
-            )
+        def level_of(u, t):
+            if u < CG:
+                return level_cols[:, u, t : t + 1]
+            return level_rest[:, u - CG, t : t + 1]
+
+        def spread_bias():
+            rows_few = bias_few[0:P:SPREAD, :].unsqueeze(1).to_broadcast([P // SPREAD, SPREAD, D])
+            nc.sync.dma_start(out=bias_rows[:], in_=rows_few)
 
         def regroup_words(u):
             u0 = max(first for first, n in X_LOADS if first <= u)
@@ -182,7 +178,7 @@ def tile_lag_channel_mixer_s4_kernel(
                         start=(k == 0),
                         stop=(k == KG - 1),
                     )
-                nc.scalar.activation(out=rows[u][:, t, h0:h1], in_=acc[:], func=RELU, bias=level_cols[:, t // 2, u, t % 2 : t % 2 + 1])
+                nc.scalar.activation(out=rows[u][:, t, h0:h1], in_=acc[:], func=RELU, bias=level_of(u, t))
 
         def interleave(copy, u, h0, h1):
             if u not in words:
@@ -243,24 +239,22 @@ def tile_lag_channel_mixer_s4_kernel(
 
         on_vector, on_scalar = nc.vector.tensor_copy, nc.scalar.copy
 
-        zero(nc.vector, level_rows[:])
-        zero(nc.vector, codes[LAST][:, 0 : BANK // 2])
         zero(nc.vector, lag_s[:].rearrange("p k n -> p (k n)"))
+        zero(nc.vector, codes[LAST][:, 0 : BANK // 2])
         zero(nc.vector, xs_raw[0][:].rearrange("p k n -> p (k n)"))
-        nc.gpsimd.dma_start(out=bias_cols[:], in_=bias.rearrange("(p c) -> p c", p=P))
-        make_identity(nc, ident[:])
+        load_level(level_first, level[0:1, :])
+        nc.gpsimd.dma_start(out=bias_few[0:P:SPREAD, :], in_=bias.partition_broadcast(P // SPREAD))
+        load_level(level_rest, level[1:B, :])
         load_x(0)
-        nc.sync.dma_start(out=level_rows[0:UNITS, :], in_=level.rearrange("b (g n) -> (b g) n", g=CG))
-        load_scale_rows(lag_s, lag_scales, 0, 1)
+        load_scale_rows(lag_s, lag_scales, 0, 2)
         nc.sync.dma_start(out=lag_w[:].bitcast(I32), in_=lag_words[:, :, :].bitcast(I32).rearrange("k p n -> p k n"))
         load_x_scales(0)
-        load_scale_rows(lag_s, lag_scales, 1, 4)
+        load_scale_rows(lag_s, lag_scales, 2, 4)
         load_x(1)
         load_x(2)
         warm_bank = psum.tile([P, BANK], F32, name="acc")
-        warm_up(warm_bank, 5)
-        turn_level()
-        spread_bias()
+        warm_up(warm_bank, 6)
+        nc.scalar.copy(out=level_cols[:], in_=level_first[:, :, 0:SLOTS])
 
         regroup_words(0)
         zero(nc.vector, xs_raw[2][:].rearrange("p k n -> p (k n)"))
@@ -269,8 +263,10 @@ def tile_lag_channel_mixer_s4_kernel(
         load_w(0)
         load_w_scales()
         load_w(1)
-        load_packed_scales()
         load_x(3)
+        load_packed_scales()
+        spread_bias()
+        load_x(4)
         regroup_scales(0, 0, 2)
         regroup_scales(0, 2, SLOTS)
         stage1(0)
@@ -282,16 +278,16 @@ def tile_lag_channel_mixer_s4_kernel(
         stage1(2)
 
         interleave(on_vector, 0, 0, HALF)
-        regroup_words(3)
-        quantise(0, 0, HALF)
         regroup_scales(3)
-        interleave(on_vector, 1, 0, HALF)
-        quantise(1, 0, HALF)
-        regroup_packed_scales()
-        load_x(4)
+        quantise(0, 0, HALF)
         interleave(on_vector, 0, HALF, H)
-        interleave(on_vector, 1, HALF, H)
+        interleave(on_vector, 1, 0, HALF)
         quantise(0, HALF, H)
+        quantise(1, 0, HALF)
+        regroup_words(3)
+        regroup_packed_scales()
+        load_x(5)
+        interleave(on_vector, 1, HALF, H)
         for g in range(CG):
             for i in range(HALF_BANKS):
                 multiply(0, i, g)

@@ -1,6 +1,7 @@
 from contextlib import ExitStack
 
 import concourse.mybir as mybir
+from concourse.masks import make_identity
 
 L, H, B, C, D = 1024, 512, 4, 1024, 1024
 FLOPS = 2 * L * H * B * C + 2 * B * H * C * D
@@ -33,7 +34,6 @@ X_LOADS = ((0, 1), (1, 1), (2, 1), (3, 1), (4, 2), (6, 2))
 XS_LOADS = ((0, 2), (2, 2))
 PACKED = 4
 V_SHARE = 128
-LEVEL_PAD = 16
 SPREAD = 8
 
 
@@ -49,7 +49,7 @@ def tile_lag_channel_mixer_s4_kernel(
         ctx.enter_context(tc.manual_schedule())
 
         def kept(shape, dtype, name):
-            return keep.tile(shape, dtype, align_bytes=64, name=name)
+            return keep.tile(shape, dtype, align_bytes=256, name=name)
 
         lag_w = kept([P, KG, 2 * H], U8, "lag_w")
         lag_s = kept([P, KG, H], U8, "lag_s")
@@ -67,9 +67,9 @@ def tile_lag_channel_mixer_s4_kernel(
         xs_late = x_pair[:].rearrange("p (u n) -> p u n", n=KG * PASS)
         codes = [kept([P, H], U32, "codes%d" % u) for u in range(UNITS)]
         code_scales = [kept([P, H], U8, "code_scales%d" % u) for u in range(UNITS)]
-        level_first = kept([P, CG, LEVEL_PAD], BF16, "level_first")
-        level_rest = kept([P, UNITS - CG, LEVEL_PAD], BF16, "level_rest")
-        level_cols = kept([P, CG, SLOTS], F32, "level_cols")
+        ident = kept([P, P], F32, "ident")
+        level_rows = kept([P, PASS], BF16, "level_rows")
+        level_cols = kept([P, 2, UNITS, 2], F32, "level_cols")
         bias_few = kept([P, D], BF16, "bias_few")
         bias_rows = kept([P, D], BF16, "bias_rows")
 
@@ -120,13 +120,14 @@ def tile_lag_channel_mixer_s4_kernel(
                     stop=True,
                 )
 
-        def load_level(dst, src):
-            nc.gpsimd.dma_start(out=dst[:, :, 0:SLOTS], in_=src.rearrange("b (g p t) -> p (b g) t", g=CG, t=SLOTS))
-
-        def level_of(u, t):
-            if u < CG:
-                return level_cols[:, u, t : t + 1]
-            return level_rest[:, u - CG, t : t + 1]
+        def turn_level():
+            pairs = level_rows[:].bitcast(F32)
+            bank = psum.tile([P, 2, P], F32, name="acc")
+            for e in range(2):
+                nc.tensor.transpose(bank[:, e, :], pairs[:, e : PASS // 2 : 2], ident[:])
+            nc.scalar.copy(
+                out=level_cols[:].rearrange("p e u i -> p e (u i)"), in_=bank[:].bitcast(BF16)[:, :, 0 : 2 * UNITS]
+            )
 
         def spread_bias():
             rows_few = bias_few[0:P:SPREAD, :].unsqueeze(1).to_broadcast([P // SPREAD, SPREAD, D])
@@ -178,7 +179,7 @@ def tile_lag_channel_mixer_s4_kernel(
                         start=(k == 0),
                         stop=(k == KG - 1),
                     )
-                nc.scalar.activation(out=rows[u][:, t, h0:h1], in_=acc[:], func=RELU, bias=level_of(u, t))
+                nc.scalar.activation(out=rows[u][:, t, h0:h1], in_=acc[:], func=RELU, bias=level_cols[:, t // 2, u, t % 2 : t % 2 + 1])
 
         def interleave(copy, u, h0, h1):
             if u not in words:
@@ -239,28 +240,29 @@ def tile_lag_channel_mixer_s4_kernel(
 
         on_vector, on_scalar = nc.vector.tensor_copy, nc.scalar.copy
 
+        zero(nc.vector, level_rows[:])
         zero(nc.vector, lag_s[:].rearrange("p k n -> p (k n)"))
         zero(nc.vector, codes[LAST][:, 0 : BANK // 2])
         zero(nc.vector, xs_raw[0][:].rearrange("p k n -> p (k n)"))
-        load_level(level_first, level[0:1, :])
-        nc.gpsimd.dma_start(out=bias_few[0:P:SPREAD, :], in_=bias.partition_broadcast(P // SPREAD))
-        load_level(level_rest, level[1:B, :])
+        make_identity(nc, ident[:])
         load_x(0)
-        load_scale_rows(lag_s, lag_scales, 0, 2)
+        nc.sync.dma_start(out=level_rows[0:UNITS, :], in_=level.rearrange("b (g n) -> (b g) n", g=CG))
+        load_scale_rows(lag_s, lag_scales, 0, 1)
         nc.sync.dma_start(out=lag_w[:].bitcast(I32), in_=lag_words[:, :, :].bitcast(I32).rearrange("k p n -> p k n"))
         load_x_scales(0)
-        load_scale_rows(lag_s, lag_scales, 2, 4)
+        load_scale_rows(lag_s, lag_scales, 1, 4)
         load_x(1)
         load_x(2)
         warm_bank = psum.tile([P, BANK], F32, name="acc")
-        warm_up(warm_bank, 6)
-        nc.scalar.copy(out=level_cols[:], in_=level_first[:, :, 0:SLOTS])
+        warm_up(warm_bank, 5)
+        turn_level()
 
         regroup_words(0)
         zero(nc.vector, xs_raw[2][:].rearrange("p k n -> p (k n)"))
         zero(nc.vector, w_s[:])
         load_x_scales(1)
         load_w(0)
+        nc.sync.dma_start(out=bias_few[0:P:SPREAD, :], in_=bias.partition_broadcast(P // SPREAD))
         load_w_scales()
         load_w(1)
         load_x(3)

@@ -78,10 +78,18 @@ def tile_lag_channel_mixer_s4_kernel(
             src = x_words[:, :, u0 * 2 * PASS : (u0 + n) * 2 * PASS].bitcast(I32)
             nc.sync.dma_start(out=x_raw[u0].bitcast(I32), in_=src.rearrange("k p n -> p k n"))
 
-        def load_scale_rows(dst, src, r0=0, r1=4):
-            for r in range(r0, r1):
+        def load_scale_rows(dst, src):
+            for r in range(4):
                 rows_r = src[:, r:16:4, :].bitcast(I32)
                 nc.sync.dma_start(out=dst[r:P:32].bitcast(I32), in_=rows_r.rearrange("k q n -> q k n"))
+
+        def load_lag_scales():
+            src = lag_scales[:, :, :].bitcast(I32).rearrange("k q n -> q k n")
+            nc.sync.dma_start(out=lag_s[0:P:8].bitcast(I32), in_=src)
+
+        def move_lag_scales():
+            for r in range(1, 4):
+                nc.sync.dma_start(out=lag_s[r:P:32].bitcast(I32), in_=lag_s[8 * r : P : 32].bitcast(I32))
 
         def load_x_scales(index):
             u0, n = XS_LOADS[index]
@@ -240,17 +248,17 @@ def tile_lag_channel_mixer_s4_kernel(
 
         on_vector, on_scalar = nc.vector.tensor_copy, nc.scalar.copy
 
-        zero(nc.vector, level_rows[:])
         zero(nc.vector, lag_s[:].rearrange("p k n -> p (k n)"))
         zero(nc.vector, codes[LAST][:, 0 : BANK // 2])
+        zero(nc.vector, level_rows[:])
         zero(nc.vector, xs_raw[0][:].rearrange("p k n -> p (k n)"))
         make_identity(nc, ident[:])
         load_x(0)
+        load_lag_scales()
         nc.sync.dma_start(out=level_rows[0:UNITS, :], in_=level.rearrange("b (g n) -> (b g) n", g=CG))
-        load_scale_rows(lag_s, lag_scales, 0, 1)
         nc.sync.dma_start(out=lag_w[:].bitcast(I32), in_=lag_words[:, :, :].bitcast(I32).rearrange("k p n -> p k n"))
         load_x_scales(0)
-        load_scale_rows(lag_s, lag_scales, 1, 4)
+        move_lag_scales()
         load_x(1)
         load_x(2)
         warm_bank = psum.tile([P, BANK], F32, name="acc")

@@ -252,12 +252,14 @@ def tile_lag_channel_mixer_s4_kernel(
         zero(nc.vector, codes[LAST][:, 0 : BANK // 2])
         zero(nc.vector, level_rows[:])
         zero(nc.vector, xs_raw[0][:].rearrange("p k n -> p (k n)"))
+        zero(nc.vector, xs_raw[2][:].rearrange("p k n -> p (k n)"))
+        zero(nc.vector, w_s[:])
         make_identity(nc, ident[:])
         load_x(0)
         load_lag_scales()
         nc.sync.dma_start(out=level_rows[0:UNITS, :], in_=level.rearrange("b (g n) -> (b g) n", g=CG))
-        nc.sync.dma_start(out=lag_w[:].bitcast(I32), in_=lag_words[:, :, :].bitcast(I32).rearrange("k p n -> p k n"))
         load_x_scales(0)
+        nc.sync.dma_start(out=lag_w[:].bitcast(I32), in_=lag_words[:, :, :].bitcast(I32).rearrange("k p n -> p k n"))
         move_lag_scales()
         load_x(1)
         load_x(2)
@@ -266,8 +268,6 @@ def tile_lag_channel_mixer_s4_kernel(
         turn_level()
 
         regroup_words(0)
-        zero(nc.vector, xs_raw[2][:].rearrange("p k n -> p (k n)"))
-        zero(nc.vector, w_s[:])
         load_x_scales(1)
         load_w(0)
         nc.sync.dma_start(out=bias_few[0:P:SPREAD, :], in_=bias.partition_broadcast(P // SPREAD))
@@ -277,8 +277,8 @@ def tile_lag_channel_mixer_s4_kernel(
         load_packed_scales()
         spread_bias()
         load_x(4)
-        regroup_scales(0, 0, 2)
-        regroup_scales(0, 2, SLOTS)
+        regroup_scales(0, 0, 1)
+        regroup_scales(0, 1, SLOTS)
         stage1(0)
         regroup_scales(1)
         regroup_words(1)

@@ -116,7 +116,7 @@ def tile_lag_channel_mixer_s4_kernel(
             engine.memset(tile.bitcast(I32), 0)
 
         def warm_up(bank, passes):
-            zeros = codes[LAST][:, 0 : BANK // 2].bitcast(U8)
+            zeros = w_s[:]
             for i in range(passes):
                 nc.tensor.matmul_mx(
                     out=bank[:],
@@ -249,12 +249,12 @@ def tile_lag_channel_mixer_s4_kernel(
         on_vector, on_scalar = nc.vector.tensor_copy, nc.scalar.copy
 
         zero(nc.vector, lag_s[:].rearrange("p k n -> p (k n)"))
-        zero(nc.vector, codes[LAST][:, 0 : BANK // 2])
+        zero(nc.vector, w_s[:])
         zero(nc.vector, level_rows[:])
         zero(nc.vector, xs_raw[0][:].rearrange("p k n -> p (k n)"))
         zero(nc.vector, xs_raw[2][:].rearrange("p k n -> p (k n)"))
-        zero(nc.vector, w_s[:])
-        make_identity(nc, ident[:])
+        zero(nc.vector, ident[:])
+        make_identity(nc, ident[:], nomemset=True)
         load_x(0)
         load_lag_scales()
         nc.sync.dma_start(out=level_rows[0:UNITS, :], in_=level.rearrange("b (g n) -> (b g) n", g=CG))

@@ -237,13 +237,14 @@ def tile_lag_channel_mixer_s4_kernel(
             y = y_tiles[b, m]
             rows_out = out[b, m * P : (m + 1) * P, :]
             width = BANK // pieces
+            last_tile = b == B - 1 and m == H // P - 1
             for c in range(pieces):
                 cols = slice(d * BANK + c * width, d * BANK + (c + 1) * width)
                 acc = banks[j, i][:, c * width : (c + 1) * width]
                 nc.vector.tensor_tensor(out=y[:, cols], in0=acc, in1=bias_rows[:, cols], op=ADD)
-                if b == B - 1:
+                if last_tile:
                     nc.sync.dma_start(out=rows_out[:, cols], in_=y[:, cols])
-            if b < B - 1 and d == DT - 1:
+            if not last_tile and d == DT - 1:
                 nc.sync.dma_start(out=rows_out, in_=y[:])
 
         on_vector, on_scalar = nc.vector.tensor_copy, nc.scalar.copy

@@ -25,9 +25,7 @@ CG = C // PASS
 UNITS = B * CG
 LAST = UNITS - 1
 BANK = 512
-DT = D // BANK
 HALF = H // 2
-HALF_BANKS = (HALF // P) * DT
 QUADS = 4
 
 X_LOADS = ((0, 1), (1, 1), (2, 1), (3, 1), (4, 2), (6, 2))
@@ -207,45 +205,39 @@ def tile_lag_channel_mixer_s4_kernel(
         banks = {}
         y_tiles = {}
 
-        def place(j, i):
-            return j // 2, (HALF // P) * (j % 2) + i // DT, i % DT
+        def groups_of(j):
+            row_tiles = range((HALF // P) * (j % 2), (HALF // P) * (j % 2 + 1))
+            return [(j // 2, m, c0, BANK) for m in row_tiles for c0 in range(0, D, BANK)]
 
-        def multiply(j, i, g):
-            b, m, d = place(j, i)
+        def multiply(group, g):
+            b, m, c0, width = group
             u = b * CG + g
             if g == 0:
-                banks[j, i] = psum.tile([P, BANK], F32, name="acc")
+                banks[group] = psum.tile([P, width], F32, name="acc")
             nc.tensor.matmul_mx(
-                out=banks[j, i][:],
+                out=banks[group][:],
                 lhsT=codes[u][:, m * P : (m + 1) * P].bitcast(FP8X4),
                 lhsT_scale=code_scales[u][:, m * P : (m + 1) * P],
-                rhs=w_w[g][:, SLOTS * d * BANK : SLOTS * (d + 1) * BANK].bitcast(FP8X4),
-                rhs_scale=w_s[4 * g : P, d * BANK : (d + 1) * BANK],
+                rhs=w_w[g][:, SLOTS * c0 : SLOTS * (c0 + width)].bitcast(FP8X4),
+                rhs_scale=w_s[4 * g : P, c0 : c0 + width],
                 start=(g == 0),
                 stop=(g == CG - 1),
             )
 
-        def stage2(j):
-            for i in range(HALF_BANKS):
+        def stage2(groups):
+            for group in groups:
                 for g in range(CG):
-                    multiply(j, i, g)
+                    multiply(group, g)
 
-        def finish(j, i, pieces=1):
-            b, m, d = place(j, i)
-            if d == 0:
+        def finish(group):
+            b, m, c0, width = group
+            if c0 == 0:
                 y_tiles[b, m] = outs.tile([P, D], F32, name="y")
             y = y_tiles[b, m]
-            rows_out = out[b, m * P : (m + 1) * P, :]
-            width = BANK // pieces
-            last_tile = b == B - 1 and m == H // P - 1
-            for c in range(pieces):
-                cols = slice(d * BANK + c * width, d * BANK + (c + 1) * width)
-                acc = banks[j, i][:, c * width : (c + 1) * width]
-                nc.vector.tensor_tensor(out=y[:, cols], in0=acc, in1=bias_rows[:, cols], op=ADD)
-                if last_tile:
-                    nc.sync.dma_start(out=rows_out[:, cols], in_=y[:, cols])
-            if not last_tile and d == DT - 1:
-                nc.sync.dma_start(out=rows_out, in_=y[:])
+            c1 = c0 + width
+            nc.vector.tensor_tensor(out=y[:, c0:c1], in0=banks[group][:], in1=bias_rows[:, c0:c1], op=ADD)
+            if c1 == D:
+                nc.sync.dma_start(out=out[b, m * P : (m + 1) * P, :], in_=y[:])
 
         on_vector, on_scalar = nc.vector.tensor_copy, nc.scalar.copy
 
@@ -300,15 +292,15 @@ def tile_lag_channel_mixer_s4_kernel(
         load_x(5)
         interleave(on_vector, 1, HALF, H)
         for g in range(CG):
-            for i in range(HALF_BANKS):
-                multiply(0, i, g)
+            for group in groups_of(0):
+                multiply(group, g)
         interleave(on_scalar, 2, 0, HALF)
         interleave(on_scalar, 2, HALF, H)
 
         for u in range(3, UNITS):
             stage1(u, 0, H if u < LAST else HALF)
-            for i in range(HALF_BANKS):
-                finish(u - 3, i)
+            for i, group in enumerate(groups_of(u - 3)):
+                finish(group)
                 if u == 3 and i == 0:
                     quantise(1, HALF, H)
             quantise(u - 1, 0, HALF)
@@ -317,32 +309,31 @@ def tile_lag_channel_mixer_s4_kernel(
                     interleave(on_vector, u - 1, H - V_SHARE, H)
                 regroup_words(u + 1)
                 quantise(u - 1, HALF, H)
-            stage2(u - 2)
+            stage2(groups_of(u - 2))
             interleave(on_scalar, u, 0, H - V_SHARE if u < LAST - 1 else HALF)
             if u >= LAST - 1:
                 h0 = HALF + (u - LAST + 1) * P
                 interleave(on_scalar, LAST - 1, h0, h0 + P)
 
         stage1(LAST, HALF, H)
-        for i in range(HALF_BANKS - 1):
-            finish(LAST - 2, i)
+        fifth, sixth, seventh = groups_of(LAST - 2), groups_of(LAST - 1), groups_of(LAST)
+        for group in fifth[:-1]:
+            finish(group)
         quantise(LAST, 0, HALF)
-        finish(LAST - 2, HALF_BANKS - 1)
+        finish(fifth[-1])
         quantise(LAST - 1, HALF, H)
-        stage2(LAST - 1)
+        stage2(sixth)
         interleave(on_scalar, LAST, HALF, HALF + P)
         interleave(on_scalar, LAST, HALF + P, H)
-        finish(LAST - 1, 0)
-        finish(LAST - 1, 1)
+        finish(sixth[0])
+        finish(sixth[1])
         quantise(LAST, HALF, HALF + P)
-        finish(LAST - 1, 2)
+        finish(sixth[2])
         quantise(LAST, HALF + P, H)
-        finish(LAST - 1, 3)
+        finish(sixth[3])
         for g in range(CG):
-            for i in range(DT):
-                multiply(LAST, i, g)
-        for i in range(DT, HALF_BANKS):
-            for g in range(CG):
-                multiply(LAST, i, g)
-        for i in range(HALF_BANKS):
-            finish(LAST, i, 2 if i == HALF_BANKS - 1 else 1)
+            for group in seventh[:2]:
+                multiply(group, g)
+        stage2(seventh[2:])
+        for group in seventh:
+            finish(group)

@@ -33,6 +33,7 @@ XS_LOADS = ((0, 2), (2, 2))
 PACKED = 4
 V_SHARE = 128
 SPREAD = 8
+NARROW = 256
 
 
 def tile_lag_channel_mixer_s4_kernel(
@@ -209,6 +210,10 @@ def tile_lag_channel_mixer_s4_kernel(
             row_tiles = range((HALF // P) * (j % 2), (HALF // P) * (j % 2 + 1))
             return [(j // 2, m, c0, BANK) for m in row_tiles for c0 in range(0, D, BANK)]
 
+        def narrow(group):
+            b, m, first, width = group
+            return [(b, m, c0, NARROW) for c0 in range(first, first + width, NARROW)]
+
         def multiply(group, g):
             b, m, c0, width = group
             u = b * CG + g
@@ -322,18 +327,16 @@ def tile_lag_channel_mixer_s4_kernel(
         quantise(LAST, 0, HALF)
         finish(fifth[-1])
         quantise(LAST - 1, HALF, H)
-        stage2(sixth)
+        opening = narrow(sixth[0]) + narrow(sixth[1])
+        stage2(opening + sixth[2:])
         interleave(on_scalar, LAST, HALF, HALF + P)
         interleave(on_scalar, LAST, HALF + P, H)
-        finish(sixth[0])
-        finish(sixth[1])
+        for group in opening:
+            finish(group)
         quantise(LAST, HALF, HALF + P)
         finish(sixth[2])
         quantise(LAST, HALF + P, H)
         finish(sixth[3])
-        for g in range(CG):
-            for group in seventh[:2]:
-                multiply(group, g)
-        stage2(seventh[2:])
         for group in seventh:
+            stage2([group])
             finish(group)

@@ -313,20 +313,24 @@ def tile_lag_channel_mixer_s4_kernel(
                 if u > 3:
                     interleave(on_vector, u - 1, H - V_SHARE, H)
                 regroup_words(u + 1)
-                quantise(u - 1, HALF, H)
+            quantise(u - 1, HALF, H)
             stage2(groups_of(u - 2))
-            interleave(on_scalar, u, 0, H - V_SHARE if u < LAST - 1 else HALF)
-            if u >= LAST - 1:
-                h0 = HALF + (u - LAST + 1) * P
-                interleave(on_scalar, LAST - 1, h0, h0 + P)
+            if u < LAST - 1:
+                interleave(on_scalar, u, 0, H - V_SHARE)
+            elif u < LAST:
+                interleave(on_scalar, u, 0, HALF)
+                interleave(on_scalar, u, HALF, H)
 
+        interleave(on_scalar, LAST, 0, P)
+        interleave(on_scalar, LAST, P, HALF)
         stage1(LAST, HALF, H)
         fifth, sixth, seventh = groups_of(LAST - 2), groups_of(LAST - 1), groups_of(LAST)
-        for group in fifth[:-1]:
-            finish(group)
-        quantise(LAST, 0, HALF)
-        finish(fifth[-1])
-        quantise(LAST - 1, HALF, H)
+        finish(fifth[0])
+        finish(fifth[1])
+        quantise(LAST, 0, P)
+        finish(fifth[2])
+        finish(fifth[3])
+        quantise(LAST, P, HALF)
         opening = narrow(sixth[0]) + narrow(sixth[1])
         stage2(opening + sixth[2:])
         interleave(on_scalar, LAST, HALF, HALF + P)

@@ -77,22 +77,22 @@ def tile_lag_channel_mixer_s4_kernel(
             src = x_words[:, :, u0 * 2 * PASS : (u0 + n) * 2 * PASS].bitcast(I32)
             nc.sync.dma_start(out=x_raw[u0].bitcast(I32), in_=src.rearrange("k p n -> p k n"))
 
-        def load_scale_rows(dst, src):
-            for r in range(4):
+        def load_scale_rows(queues, dst, src):
+            for r, queue in enumerate(queues):
                 rows_r = src[:, r:16:4, :].bitcast(I32)
-                nc.sync.dma_start(out=dst[r:P:32].bitcast(I32), in_=rows_r.rearrange("k q n -> q k n"))
+                queue.dma_start(out=dst[r:P:32].bitcast(I32), in_=rows_r.rearrange("k q n -> q k n"))
 
         def load_lag_scales():
             src = lag_scales[:, :, :].bitcast(I32).rearrange("k q n -> q k n")
             nc.sync.dma_start(out=lag_s[0:P:8].bitcast(I32), in_=src)
 
         def move_lag_scales():
-            for r in range(1, 4):
-                nc.sync.dma_start(out=lag_s[r:P:32].bitcast(I32), in_=lag_s[8 * r : P : 32].bitcast(I32))
+            for r, queue in ((1, nc.sync), (2, nc.scalar), (3, nc.sync)):
+                queue.dma_start(out=lag_s[r:P:32].bitcast(I32), in_=lag_s[8 * r : P : 32].bitcast(I32))
 
-        def load_x_scales(index):
+        def load_x_scales(index, queues):
             u0, n = XS_LOADS[index]
-            load_scale_rows(xs_raw[u0], x_scales[:, :, u0 * PASS : (u0 + n) * PASS])
+            load_scale_rows(queues, xs_raw[u0], x_scales[:, :, u0 * PASS : (u0 + n) * PASS])
 
         def load_packed_scales():
             for k in range(KG):
@@ -256,7 +256,7 @@ def tile_lag_channel_mixer_s4_kernel(
         load_x(0)
         load_lag_scales()
         nc.sync.dma_start(out=level_rows[0:UNITS, :], in_=level.rearrange("b (g n) -> (b g) n", g=CG))
-        load_x_scales(0)
+        load_x_scales(0, [nc.sync] + [nc.scalar] * 3)
         nc.sync.dma_start(out=lag_w[:].bitcast(I32), in_=lag_words[:, :, :].bitcast(I32).rearrange("k p n -> p k n"))
         move_lag_scales()
         load_x(1)
@@ -266,7 +266,7 @@ def tile_lag_channel_mixer_s4_kernel(
         turn_level()
 
         regroup_words(0)
-        load_x_scales(1)
+        load_x_scales(1, [nc.sync] * 4)
         load_w(0)
         nc.sync.dma_start(out=bias_few[0:P:SPREAD, :], in_=bias.partition_broadcast(P // SPREAD))
         load_w_scales()

from contextlib import ExitStack

import concourse.mybir as mybir
from concourse.masks import make_identity

L, H, B, C, D = 1024, 512, 4, 1024, 1024
FLOPS = 2 * L * H * B * C + 2 * B * H * C * D

F32 = mybir.dt.float32
BF16 = mybir.dt.bfloat16
I32 = mybir.dt.int32
U32 = mybir.dt.uint32
U16 = mybir.dt.uint16
U8 = mybir.dt.uint8
FP4X4 = mybir.dt.float4_e2m1fn_x4
FP8X4 = mybir.dt.float8_e4m3fn_x4
ADD = mybir.AluOpType.add
RELU = mybir.ActivationFunctionType.Relu

P = 128
SLOTS = 4
PASS = P * SLOTS
KG = L // PASS
CG = C // PASS
UNITS = B * CG
LAST = UNITS - 1
BANK = 512
HALF = H // 2
QUADS = 4

X_LOADS = ((0, 1), (1, 1), (2, 1), (3, 1), (4, 2), (6, 2))
XS_LOADS = ((0, 2), (2, 2))
PACKED = 4
V_SHARE = 128
SPREAD = 8
NARROW = 256


def tile_lag_channel_mixer_s4_kernel(
    tc, lag_words, lag_scales, x_words, x_scales, w_words, w_scales, level, bias, out
):
    nc = tc.nc
    with ExitStack() as ctx:
        keep = ctx.enter_context(tc.tile_pool(name="keep", bufs=1))
        work = ctx.enter_context(tc.tile_pool(name="work", bufs=3))
        outs = ctx.enter_context(tc.tile_pool(name="outs", bufs=8))
        psum = ctx.enter_context(tc.psum_pool(name="psum", bufs=8))
        ctx.enter_context(tc.manual_schedule())

        def kept(shape, dtype, name):
            return keep.tile(shape, dtype, align_bytes=256, name=name)

        lag_w = kept([P, KG, 2 * H], U8, "lag_w")
        lag_s = kept([P, KG, H], U8, "lag_s")
        w_w = [kept([P, SLOTS * D], U8, "w_w%d" % g) for g in range(CG)]
        w_s = kept([P, D], U8, "w_s")
        x_raw = {u0: kept([P, KG, n * 2 * PASS], U8, "x_raw%d" % u0)[:] for u0, n in X_LOADS if u0 not in (2, 3)}
        x_pair = kept([P, 2 * KG * 2 * PASS], U8, "x_pair")
        for u in (2, 3):
            x_raw[u] = x_pair[:, (u - 2) * KG * 2 * PASS : (u - 1) * KG * 2 * PASS].rearrange("p (k n) -> p k n", k=KG)
        x_st = [kept([P, SLOTS, KG, 2 * P], U8, "x_st%d" % u) for u in range(UNITS)]
        xs_raw = {u0: kept([P, KG, n * PASS], U8, "xs_raw%d" % u0) for u0, n in XS_LOADS}
        xs_st = [kept([P, SLOTS, KG, P], U8, "xs_st%d" % u) for u in range(PACKED)]
        packed_raw = kept([P, PASS], U8, "packed_raw")
        packed_st = kept([P, SLOTS, P], U8, "packed_st")
        xs_late = x_pair[:].rearrange("p (u n) -> p u n", n=KG * PASS)
        codes = [kept([P, H], U32, "codes%d" % u) for u in range(UNITS)]
        code_scales = [kept([P, H], U8, "code_scales%d" % u) for u in range(UNITS)]
        ident = kept([P, P], F32, "ident")
        level_rows = kept([P, PASS], BF16, "level_rows")
        level_cols = kept([P, 2, UNITS, 2], F32, "level_cols")
        bias_few = kept([P, D], BF16, "bias_few")
        bias_rows = kept([P, D], BF16, "bias_rows")

        def load_x(index):
            u0, n = X_LOADS[index]
            src = x_words[:, :, u0 * 2 * PASS : (u0 + n) * 2 * PASS].bitcast(I32)
            nc.sync.dma_start(out=x_raw[u0].bitcast(I32), in_=src.rearrange("k p n -> p k n"))

        def load_scale_rows(queues, dst, src):
            for r, queue in enumerate(queues):
                rows_r = src[:, r:16:4, :].bitcast(I32)
                queue.dma_start(out=dst[r:P:32].bitcast(I32), in_=rows_r.rearrange("k q n -> q k n"))

        def load_lag_scales():
            src = lag_scales[:, :, :].bitcast(I32).rearrange("k q n -> q k n")
            nc.sync.dma_start(out=lag_s[0:P:8].bitcast(I32), in_=src)

        def move_lag_scales():
            for r, queue in ((1, nc.sync), (2, nc.scalar), (3, nc.sync)):
                queue.dma_start(out=lag_s[r:P:32].bitcast(I32), in_=lag_s[8 * r : P : 32].bitcast(I32))

        def load_x_scales(index, queues):
            u0, n = XS_LOADS[index]
            load_scale_rows(queues, xs_raw[u0], x_scales[:, :, u0 * PASS : (u0 + n) * PASS])

        def load_packed_scales():
            for k in range(KG):
                rows_k = x_scales[k, :, PACKED * PASS : UNITS * PASS].bitcast(I32)
                nc.sync.dma_start(
                    out=packed_raw[k:P:KG, :].bitcast(I32), in_=rows_k.rearrange("q (u n) -> q u n", u=UNITS - PACKED)
                )

        def load_w(g):
            nc.sync.dma_start(out=w_w[g][:].bitcast(I32), in_=w_words[g].rearrange("p n t -> p (n t)").bitcast(I32))

        def load_w_scales():
            for q in range(QUADS):
                nc.sync.dma_start(
                    out=w_s[32 * q : 32 * q + 4 * CG, :].bitcast(I32),
                    in_=w_scales[:, 4 * q : 4 * q + 4, :].bitcast(I32),
                )

        def zero(engine, tile):
            engine.memset(tile.bitcast(I32), 0)

        def warm_up(bank, passes):
            zeros = w_s[:]
            for i in range(passes):
                nc.tensor.matmul_mx(
                    out=bank[:],
                    lhsT=zeros[:, 0 : 2 * P].bitcast(FP4X4),
                    lhsT_scale=zeros[:, 0:P],
                    rhs=zeros.bitcast(FP4X4),
                    rhs_scale=zeros[:, 0:BANK],
                    start=True,
                    stop=True,
                )

        def turn_level():
            pairs = level_rows[:].bitcast(F32)
            bank = psum.tile([P, 2, P], F32, name="acc")
            for e in range(2):
                nc.tensor.transpose(bank[:, e, :], pairs[:, e : PASS // 2 : 2], ident[:])
            nc.scalar.copy(
                out=level_cols[:].rearrange("p e u i -> p e (u i)"), in_=bank[:].bitcast(BF16)[:, :, 0 : 2 * UNITS]
            )

        def spread_bias():
            rows_few = bias_few[0:P:SPREAD, :].unsqueeze(1).to_broadcast([P // SPREAD, SPREAD, D])
            nc.sync.dma_start(out=bias_rows[:], in_=rows_few)

        def regroup_words(u):
            u0 = max(first for first, n in X_LOADS if first <= u)
            raw = x_raw[u0][:, :, (u - u0) * 2 * PASS : (u - u0 + 1) * 2 * PASS].bitcast(U16)
            nc.vector.tensor_copy(
                out=x_st[u][:].bitcast(U16).rearrange("p t k (c i) -> p k c t i", i=8),
                in_=raw.rearrange("p k (c i t) -> p k c t i", i=8, t=SLOTS),
            )

        def regroup_scales(u, t0=0, t1=SLOTS):
            u0 = max(first for first, n in XS_LOADS if first <= u)
            raw = xs_raw[u0][:, :, (u - u0) * PASS : (u - u0 + 1) * PASS]
            nc.vector.tensor_copy(
                out=xs_st[u][:, t0:t1], in_=raw.rearrange("p k (m t) -> p t k m", t=SLOTS)[:, t0:t1]
            )

        def regroup_packed_scales():
            nc.vector.tensor_copy(out=packed_st[:], in_=packed_raw[:].rearrange("p (m t) -> p t m", t=SLOTS))
            for q in (0, 2, 1, 3):
                nc.sync.dma_start(
                    out=xs_late[32 * q : 32 * q + 4].rearrange("p u (k n) -> p (u k) n", k=KG).bitcast(I32),
                    in_=packed_st[32 * q : 32 * q + 32].rearrange("p t m -> p (t m)").bitcast(I32),
                )

        def x_scale(u, k, t):
            if u < PACKED:
                return xs_st[u][:, t, k, :]
            return xs_late[:, u - PACKED, k * PASS + t * P : k * PASS + (t + 1) * P]

        rows = {}
        words = {}

        def stage1(u, h0=0, h1=H):
            if u not in rows:
                rows[u] = work.tile([P, SLOTS, H], BF16, align_bytes=64, name="rows")
            for t in range(SLOTS):
                acc = psum.tile([P, h1 - h0], F32, name="acc")
                for k in range(KG):
                    nc.tensor.matmul_mx(
                        out=acc[:],
                        lhsT=x_st[u][:, t, k, :].bitcast(FP4X4),
                        lhsT_scale=x_scale(u, k, t),
                        rhs=lag_w[:, k, 2 * h0 : 2 * h1].bitcast(FP4X4),
                        rhs_scale=lag_s[:, k, h0:h1],
                        start=(k == 0),
                        stop=(k == KG - 1),
                    )
                nc.scalar.activation(out=rows[u][:, t, h0:h1], in_=acc[:], func=RELU, bias=level_cols[:, t // 2, u, t % 2 : t % 2 + 1])

        def interleave(copy, u, h0, h1):
            if u not in words:
                words[u] = work.tile([P, H, SLOTS], BF16, align_bytes=64, name="words")
            copy(
                out=words[u][:, h0:h1, :].rearrange("p (c i) t -> p c t i", i=4),
                in_=rows[u][:, :, h0:h1].rearrange("p t (c i) -> p c t i", i=4),
            )

        def quantise(u, h0, h1):
            nc.vector.quantize_mx(
                out=codes[u][:, h0:h1].bitcast(FP8X4),
                scales=code_scales[u][:, h0:h1],
                in_=words[u][:, h0:h1, :].rearrange("p h t -> p (h t)"),
            )

        banks = {}
        y_tiles = {}

        def groups_of(j):
            row_tiles = range((HALF // P) * (j % 2), (HALF // P) * (j % 2 + 1))
            return [(j // 2, m, c0, BANK) for m in row_tiles for c0 in range(0, D, BANK)]

        def narrow(group):
            b, m, first, width = group
            return [(b, m, c0, NARROW) for c0 in range(first, first + width, NARROW)]

        def multiply(group, g):
            b, m, c0, width = group
            u = b * CG + g
            if g == 0:
                banks[group] = psum.tile([P, width], F32, name="acc")
            nc.tensor.matmul_mx(
                out=banks[group][:],
                lhsT=codes[u][:, m * P : (m + 1) * P].bitcast(FP8X4),
                lhsT_scale=code_scales[u][:, m * P : (m + 1) * P],
                rhs=w_w[g][:, SLOTS * c0 : SLOTS * (c0 + width)].bitcast(FP8X4),
                rhs_scale=w_s[4 * g : P, c0 : c0 + width],
                start=(g == 0),
                stop=(g == CG - 1),
            )

        def stage2(groups):
            for group in groups:
                for g in range(CG):
                    multiply(group, g)

        def finish(group):
            b, m, c0, width = group
            if c0 == 0:
                y_tiles[b, m] = outs.tile([P, D], F32, name="y")
            y = y_tiles[b, m]
            c1 = c0 + width
            nc.vector.tensor_tensor(out=y[:, c0:c1], in0=banks[group][:], in1=bias_rows[:, c0:c1], op=ADD)
            if c1 == D:
                nc.sync.dma_start(out=out[b, m * P : (m + 1) * P, :], in_=y[:])

        on_vector, on_scalar = nc.vector.tensor_copy, nc.scalar.copy

        zero(nc.vector, lag_s[:].rearrange("p k n -> p (k n)"))
        zero(nc.vector, w_s[:])
        zero(nc.vector, level_rows[:])
        zero(nc.vector, xs_raw[0][:].rearrange("p k n -> p (k n)"))
        zero(nc.vector, xs_raw[2][:].rearrange("p k n -> p (k n)"))
        zero(nc.vector, ident[:])
        make_identity(nc, ident[:], nomemset=True)
        load_x(0)
        load_lag_scales()
        nc.sync.dma_start(out=level_rows[0:UNITS, :], in_=level.rearrange("b (g n) -> (b g) n", g=CG))
        load_x_scales(0, [nc.sync] + [nc.scalar] * 3)
        nc.sync.dma_start(out=lag_w[:].bitcast(I32), in_=lag_words[:, :, :].bitcast(I32).rearrange("k p n -> p k n"))
        move_lag_scales()
        load_x(1)
        load_x(2)
        warm_bank = psum.tile([P, BANK], F32, name="acc")
        warm_up(warm_bank, 5)
        turn_level()

        regroup_words(0)
        load_x_scales(1, [nc.sync] * 4)
        load_w(0)
        nc.sync.dma_start(out=bias_few[0:P:SPREAD, :], in_=bias.partition_broadcast(P // SPREAD))
        load_w_scales()
        load_w(1)
        load_x(3)
        load_packed_scales()
        spread_bias()
        load_x(4)
        regroup_scales(0, 0, 1)
        regroup_scales(0, 1, SLOTS)
        stage1(0)
        regroup_scales(1)
        regroup_words(1)
        stage1(1)
        regroup_words(2)
        regroup_scales(2)
        stage1(2)

        interleave(on_vector, 0, 0, HALF)
        regroup_scales(3)
        quantise(0, 0, HALF)
        interleave(on_vector, 0, HALF, H)
        interleave(on_vector, 1, 0, HALF)
        quantise(0, HALF, H)
        quantise(1, 0, HALF)
        regroup_words(3)
        regroup_packed_scales()
        load_x(5)
        interleave(on_vector, 1, HALF, H)
        for g in range(CG):
            for group in groups_of(0):
                multiply(group, g)
        interleave(on_scalar, 2, 0, HALF)
        interleave(on_scalar, 2, HALF, H)

        for u in range(3, UNITS):
            stage1(u, 0, H if u < LAST else HALF)
            for i, group in enumerate(groups_of(u - 3)):
                finish(group)
                if u == 3 and i == 0:
                    quantise(1, HALF, H)
            quantise(u - 1, 0, HALF)
            if u < LAST:
                if u > 3:
                    interleave(on_vector, u - 1, H - V_SHARE, H)
                regroup_words(u + 1)
            quantise(u - 1, HALF, H)
            stage2(groups_of(u - 2))
            if u < LAST - 1:
                interleave(on_scalar, u, 0, H - V_SHARE)
            elif u < LAST:
                interleave(on_scalar, u, 0, HALF)
                interleave(on_scalar, u, HALF, H)

        interleave(on_scalar, LAST, 0, P)
        interleave(on_scalar, LAST, P, HALF)
        stage1(LAST, HALF, H)
        fifth, sixth, seventh = groups_of(LAST - 2), groups_of(LAST - 1), groups_of(LAST)
        finish(fifth[0])
        finish(fifth[1])
        quantise(LAST, 0, P)
        finish(fifth[2])
        finish(fifth[3])
        quantise(LAST, P, HALF)
        opening = narrow(sixth[0]) + narrow(sixth[1])
        stage2(opening + sixth[2:])
        interleave(on_scalar, LAST, HALF, HALF + P)
        interleave(on_scalar, LAST, HALF + P, H)
        for group in opening:
            finish(group)
        quantise(LAST, HALF, HALF + P)
        finish(sixth[2])
        quantise(LAST, HALF + P, H)
        finish(sixth[3])
        for group in seventh:
            stage2([group])
            finish(group)
